import numpy as np, ml_dtypes
CORES = [3,11,19,27,35,43,51,59]
N = 8
BF = ml_dtypes.bfloat16
W, L, RO, PX, LIM = 4096, 128, 4, 2, 11
def parts(rng):
    X = rng.integers(0, 64, (N, 8, 16, W)); H = rng.integers(0, 2 * W, (N, 8, 16, L)); c = rng.integers(0, W, (N, 8, L)); z = rng.integers(0, 64, (N, 8, 16, L))
    return X, H, c, z, np.argsort(rng.random((N, 8, W)), axis=-1).astype(np.int64)
def pack(X, H, c, z, nx):
    return {"xt": np.ascontiguousarray(X.reshape(N, 128, W)).astype(np.float32).astype(BF), "mem": np.ascontiguousarray(H.reshape(N, 128, L)).astype(np.int32),
            "plc": np.ascontiguousarray(c).astype(np.int32), "zt": np.ascontiguousarray(z.reshape(N, 128, L)).astype(np.float32).astype(BF), "nxt": np.ascontiguousarray(nx).astype(np.int32)}
def choose(X, H, c, z, pen):
    e = H >> 1; d = np.where((H & 1) == 1, -e, e); cc = c[:, :, None, :]
    pl = np.concatenate([(cc + d) % W, (cc - d) % W], axis=2); co = []
    for h in (0, 1):
        v = np.take_along_axis(X, np.ascontiguousarray(pl[:, :, 16 * h:16 * h + 16]).reshape(N, 8, 1, 16 * L), 3).reshape(N, 8, 16, 16, L)
        co.append(np.add.reduce(np.abs(v - z[:, :, :, None, :]), axis=2) + 4 * np.arange(16)[:, None] + h * pen[:, None, None, None])
    return pl, np.argmin(np.concatenate(co, axis=2), axis=2)
def setup_inputs(rng):
    return pack(*parts(rng))
def setup_inputs_corners(rng):
    X, H, c, z, nx = parts(rng); far = np.array([0, 1, W // 2 - 1, W // 2, W // 2 + 1, W - 1]); spots = np.array([0, 1, W // 2, W - 1])
    for p in range(N):
        for g in range(8):
            k = (p + g) % 8
            if k == 0: H[p, g] = 2 * rng.choice(far, (16, L)) + rng.integers(0, 2, (16, L)); c[p, g] = rng.choice(spots, L)
            if k == 1: H[p, g] = H[p, g, :1].copy()
            if k == 2: H[p, g] = 2 * (H[p, g, :1] >> 1) + (np.arange(16) % 2)[:, None]
            if k == 3: nx[p, g] = np.arange(W); c[p, g] = rng.choice(spots, L)
            if k == 4: nx[p, g] = rng.choice(np.array([0, W - 1]), W)
            if k == 5: nx[p, g] = (np.arange(W) + 1) % W; H[p, g] = rng.integers(0, 4, (16, L))
            if k == 6: H[p, g] = np.where(rng.random((1, L)) < 0.5, 0, 2 * W - 1)
            if k == 7: c[p, g] = rng.choice(spots, L); X[p, g] = rng.integers(0, 64, (16, 3))[:, rng.integers(0, 3, W)]
    return pack(X, H, c, z, nx)
def setup_inputs_crowd(rng):
    X, H, c, z, nx = parts(rng); few = int(rng.integers(1, 4))
    for p in range(N):
        for g in range(8):
            P = rng.permutation(np.arange(1, W - 1))[:3]; k = (p + g) % 5
            if g % 4 == 0: P[0] = 0
            if g % 4 == 3: P[0] = W - 1
            near = p >= N - 2 and g == (-p) % 5
            if near:
                x0 = np.full(16, 32) if p == N - 2 else X[p, g][:, P[0]].copy()
                far = np.full(16, 62) if p == N - 2 else np.minimum((x0 + 32) % 64, 62)
                X[p, g] = far[:, None] + rng.integers(0, 2, (16, W)) * (np.arange(16) < 4)[:, None]; X[p, g, :, P[0]] = x0
            to = np.full(L, P[0])
            if k == 1: to[0] = P[1]
            if k == 2: to[L - 1] = P[1]
            if k == 3: to = P[rng.integers(0, 3, L)]
            if k == 4: to = rng.permutation(W)[:L]
            if p == N - 2:
                H[p, g] = rng.integers(0, 2, (16, L)); c[p, g] = to; z[p, g] = np.where(X[p, g][:, to] < 32, 63, 0)
                if near:
                    for i in (L - 1, 0, L // 2)[:few]:
                        e = int(rng.integers(1, W // 2)); s = int(rng.integers(0, 2))
                        H[p, g, 0, i] = 2 * e + s; c[p, g, i] = (P[0] + (-e if s == 1 else e)) % W
                continue
            rev = np.full(L, 1) if p in (0, N - 1) else (rng.permutation(L) < L // 2 - int(g == 7)).astype(np.int64)
            if p == N - 1 and g == 7: rev[L - 1] = 0
            e = rng.integers(1, W // 2, L); s = rng.integers(0, 2, L); d = np.where(s == 1, -e, e)
            c[p, g] = (to + np.where(rev == 1, d, -d)) % W; H[p, g, 0] = 2 * e + s
            z[p, g] = np.clip(X[p, g][:, to] + rng.integers(-2, 3, (16, L)), 0, 63)
    return pack(X, H, c, z, nx)
def setup_inputs_ends(rng):
    X = np.where(rng.random((N, 8, 1, W)) < 0.5, 63 * rng.integers(0, 2, (N, 8, 1, W)), 63 * rng.integers(0, 2, (N, 8, 16, W)))
    z = np.where(rng.random((N, 8, 1, L)) < 0.5, 63 * rng.integers(0, 2, (N, 8, 1, L)), 63 * rng.integers(0, 2, (N, 8, 16, L)))
    H = (2 * W - 1) * rng.integers(0, 2, (N, 8, 16, L)); c = (W - 1) * rng.integers(0, 2, (N, 8, L)); nx = (W - 1) * rng.integers(0, 2, (N, 8, W))
    o = rng.integers(0, 2, (N, 8)); o[:, 7] = 1; nx[:, :, 0] = (W - 1) * o; nx[:, :, W - 1] = (W - 1) * (1 - o)
    for q in (0, 1, W - 2, W - 1):
        X[:, 1, :, q] = 63; X[:, 6, :, q] = 0; X[:, 7, :, q] = 0 if q < 2 else 63
    z[:, 1] = 63 * rng.integers(0, 2, (N, 1, L)); z[:, 6] = 63 * rng.integers(0, 2, (N, 1, L))
    for i in (0, 1, L - 1): z[:, 1, :, i] = 0; z[:, 6, :, i] = 63
    rest = np.add.reduce((choose(X, H, c, z, np.zeros(N, np.int64))[1] >> 4)[:, :7].reshape(N, -1), axis=1)
    for p in range(N):
        n = 32 + ((0 if p == 1 else 31) - int(rest[p])) % 32
        m = np.zeros(L, bool); m[0] = True; m[L - 1] = True; m[rng.permutation(np.arange(1, L - 1))[:n - 2]] = True
        cc = (W - 1) * rng.integers(0, 2, L); cc[m] = 0; zz = 63 * rng.integers(0, 2, L); zz[m] = 63; zz[(~m) & (cc == 0)] = 0
        c[p, 7] = cc; z[p, 7] = zz[None, :]; H[p, 7, 0] = np.where(m | (zz == 0), 2 * W - 1, 0)
        for i in (0, L - 1): H[p, 7, 12:, i] = 2 * W - 1
    return pack(X, H, c, z, nx)
def setup_inputs_spread(rng):
    X = np.minimum((np.exp2(6 * rng.random((N, 8, 1, W))) * rng.random((N, 8, 16, W))).astype(np.int64), 63)
    z = np.minimum((np.exp2(6 * rng.random((N, 8, 1, L))) * rng.random((N, 8, 16, L))).astype(np.int64), 63)
    e = np.clip(np.power(float(W), rng.random((N, 8, 16, L))).astype(np.int64) - 1, 0, W - 1)
    H = 2 * e + (rng.random((N, 8, 16, L)) < rng.random((N, 8, 1, 1))).astype(np.int64)
    c = np.minimum((W * rng.random((N, 8, L)) ** 3).astype(np.int64), W - 1); nx = np.minimum((W * rng.random((N, 8, W)) ** 2).astype(np.int64), W - 1)
    return pack(X, H, c, z, nx)
def setup_inputs_ties(rng):
    X, H, c, z, nx = parts(rng)
    X[:, 2:7] = 4 * rng.integers(0, 12, (N, 1, 16, 1)) + 4 * rng.integers(0, 3, (N, 5, 16, W)) * (np.arange(16) < 2)[:, None]
    z[:, 2:7] = 4 * rng.integers(0, 16, (N, 5, 16, L)); X[:, 7] = rng.integers(0, 64, (N, 16, 1)); X[:, :2] = 0
    X[:, 6] = 63 - (np.argsort(rng.random((N, 16, W)), axis=1) < rng.integers(0, 9, (N, 1, W))).astype(np.int64); z[:, 6] = 0
    o = N - 1 if PX < N - 1 else PX - 1
    X[o, 6] = 63 - X[o, 6]
    for p in range(N):
        if p < (p ^ PX):
            lo = rng.integers(0, 63 - LIM, (2, 16, L)); n = rng.choice(np.array([0, 7, 8, 9, 10, 16]), (2, 1, L))
            hi = lo + np.where(np.argsort(rng.random((2, 16, L)), axis=1) < n, LIM, LIM + 1); sw = rng.random((2, 1, L)) < 0.5
            z[p, :2] = np.where(sw, hi, lo); z[p ^ PX, :2] = np.where(sw, lo, hi)
    return pack(X, H, c, z, nx)
def check_inputs(d):
    bad = []
    for k, hi in (("xt", 63), ("mem", 2 * W - 1), ("plc", W - 1), ("zt", 63), ("nxt", W - 1)):
        v = np.asarray(d[k]).astype(np.float64)
        if not (np.min(v) >= 0 and np.max(v) <= hi): bad.append("range of " + k)
        elif np.any(v != np.floor(v)): bad.append("whole numbers in " + k)
    return bad
def reference(xt, mem, plc, zt, nxt):
    X = xt.astype(np.float32).astype(np.int64).reshape(N, 8, 16, W); nx = nxt.astype(np.int64)
    H = mem.astype(np.int64).reshape(N, 8, 16, L); c = plc.astype(np.int64); z = zt.astype(np.float32).astype(np.int64).reshape(N, 8, 16, L)
    A = np.zeros(N, np.int64); par = np.arange(N) ^ PX
    for t in range(RO):
        if t > 0: H = np.roll(H, 1, axis=0); c = np.roll(c, 1, axis=0); z = np.roll(z, 1, axis=0)
        pl, w = choose(X, H, c, z, A & 31); rev = w >> 4
        q = np.take_along_axis(pl, w[:, :, None, :], 2)[:, :, 0]
        step = np.take_along_axis(H, (w & 15)[:, :, None, :], 2) ^ rev[:, :, None, :]
        A = np.add.reduce(rev.reshape(N, -1), axis=1)
        xq = np.take_along_axis(X, q[:, :, None, :], 3); half = (xq + z) >> 1
        u, first = np.unique((np.arange(N * 8).reshape(N, 8, 1) * W + q).reshape(-1), return_index=True)
        X[u // (8 * W), (u // W) % 8, :, u % W] = half.transpose(0, 1, 3, 2).reshape(-1, 16)[first]
        z = np.abs(z - xq); c = np.take_along_axis(nx, q, 2)
        H = np.concatenate([step, H[:, :, :15]], axis=2)
        alike = np.add.reduce((np.abs(z - z[par]) <= LIM).astype(np.int64), axis=2) >= 9
        H = np.concatenate([H[:, :, :8], np.where(alike[:, :, None, :], H[par][:, :, 8:], H[:, :, 8:])], axis=2)
    return {"yx": X.reshape(N, 128, W).astype(np.float32).astype(BF), "yh": H.reshape(N, 128, L).astype(np.float32), "yc": c.astype(np.float32), "yz": z.reshape(N, 128, L).astype(np.float32).astype(BF)}

@@ -1,0 +1,598 @@
+from concourse.mybir import AluOpType as OP, ActivationFunctionType as AF
+
+N, W, RO, PX, LIM = 8, 4096, 4, 2, 11
+TRI = [8 * s * (s + 1) for s in range(9)]
+STEP, FAR = 16384.0, 4194304.0
+
+SCRATCH = {
+    "X": ("sbuf", [128, 2 * W + 384], "bfloat16"),
+    "NX": ("sbuf", [128, W], "float32"), "IO": ("sbuf", [128, W], "float32"),
+    "nxi": ("sbuf", [128, 256], "int32"), "nxh": ("sbuf", [128, 256], "float16"),
+    "LP": ("sbuf", [128, 2048], "float16"),
+    "mi": ("sbuf", [128, 128], "int32"), "pli": ("sbuf", [128, 128], "int32"), "plf": ("sbuf", [128, 128], "float32"),
+    "J1": ("sbuf", [128, 128], "int32"), "J2": ("sbuf", [128, 128], "int32"), "J3": ("sbuf", [128, 144], "int32"),
+    "J4": ("sbuf", [128, 128], "int32"), "G8": ("sbuf", [128, 128], "float32"),
+    "ta": ("sbuf", [128, 256], "int32"), "tb": ("sbuf", [128, 256], "int32"), "tc": ("sbuf", [128, 16], "int32"),
+    "fa": ("sbuf", [128, 256], "float32"), "fb": ("sbuf", [128, 256], "float32"), "fc": ("sbuf", [128, 256], "float32"),
+    "CI": ("sbuf", [128, 8], "int32"), "CF": ("sbuf", [128, 24], "float32"),
+    "Ib": ("sbuf", [128, 128], "bfloat16"), "nIb": ("sbuf", [128, 128], "bfloat16"),
+    "If": ("sbuf", [128, 128], "float32"), "nIf": ("sbuf", [128, 128], "float32"),
+    "MK": ("sbuf", [128, 128], "bfloat16"), "KP": ("sbuf", [128, 128], "bfloat16"),
+    "BO": ("sbuf", [128, 128], "bfloat16"), "ZR": ("sbuf", [128, 256], "bfloat16"), "GS": ("sbuf", [128, 40], "bfloat16"),
+    "WD": ("sbuf", [128, 144], "bfloat16"),
+    "D0": ("sbuf", [128, 256], "float32"), "DD": ("sbuf", [128, 576], "bfloat16"), "DUM": ("sbuf", [128, 16], "float32"),
+    "LS": ("sbuf", [128, 96], "uint16"), "OFF": ("sbuf", [128, 256], "uint16"),
+    "DA": ("sbuf", [128, 2048], "bfloat16"), "AD": ("sbuf", [128, 2048], "bfloat16"),
+    "XB": ("sbuf", [128, 2048], "bfloat16"), "MB": ("sbuf", [128, 2048], "bfloat16"),
+    "SC": ("sbuf", [128, 256], "int32"), "C31": ("sbuf", [128, 256], "bfloat16"), "IDX": ("sbuf", [128, 8], "int32"),
+    "LT": ("sbuf", [128, 128], "bfloat16"), "WO": ("sbuf", [128, 8], "uint16"),
+    "G1": ("sbuf", [128, 128], "float32"), "G2": ("sbuf", [128, 128], "float32"), "SS": ("sbuf", [128, 256], "float32"),
+    "Q1": ("sbuf", [128, 8], "int32"), "Q2": ("sbuf", [128, 8], "int32"), "QO": ("sbuf", [128, 8], "uint16"),
+    "XQ": ("sbuf", [128, 128], "bfloat16"), "DQ": ("sbuf", [128, 128], "bfloat16"),
+    "T1": ("sbuf", [128, 128], "bfloat16"), "ZM": ("sbuf", [128, 128], "bfloat16"),
+    "QN": ("sbuf", [128, 128], "float32"), "QF": ("sbuf", [128, 8], "float32"), "NB": ("sbuf", [128, 8], "float32"),
+    "QR": ("sbuf", [128, 16], "float32"),
+    "E": ("sbuf", [128, 576], "bfloat16"), "ES": ("sbuf", [128, 576], "bfloat16"),
+    "LO": ("sbuf", [128, 16], "float32"), "LO2": ("sbuf", [128, 16], "float32"), "SO": ("sbuf", [128, 16], "uint16"),
+    "H8": ("sbuf", [128, 8], "bfloat16"), "PN": ("sbuf", [128, 8], "float32"), "PI": ("sbuf", [128, 8], "int32"),
+    "DIF": ("sbuf", [128, 64], "float32"), "TT": ("sbuf", [128, 64], "float32"),
+    "AB": ("sbuf", [128, 128], "bfloat16"), "S1": ("sbuf", [128, 128], "bfloat16"),
+    "SG": ("sbuf", [128, 8], "float32"), "AL": ("sbuf", [128, 8], "float32"),
+    "YC": ("sbuf", [128, 128], "float32"), "YH": ("sbuf", [128, 128], "float32"), "U": ("sbuf", [128, 192], "float32"),
+}
+for _t in range(RO + 1):
+    SCRATCH["W%d" % _t] = ("sbuf", [128, 264], "float32")
+    if _t > 0:
+        SCRATCH["PA%d" % _t] = ("sbuf", [128, 64], "float32")
+        SCRATCH["PZ%d" % _t] = ("sbuf", [128, 128], "bfloat16")
+    if _t < RO:
+        SCRATCH["M%d" % _t] = ("sbuf", [128, 608], "bfloat16")
+        SCRATCH["O%d" % _t] = ("sbuf", [128, 224], "bfloat16")
+PSUM = ["P", "ZP", "F1a", "F1b", "F2a", "F2b", "EX", "WL"]
+for _n in PSUM:
+    SCRATCH[_n] = ("psum", [128, 512], "float32")
+
+DMAS = ["dmem", "dplc", "dz", "dnx", "dx1", "dx2", "dyz", "dyc", "dyx", "dyh"]
+SEMAPHORES = ["qv", "qs", "qp", "qg", "snt"] + DMAS + [k + str(t) for t in range(1, RO + 1) for k in ("am", "az", "ae", "ap")]
+
+L_TILE, L_REP, L_MSG, L_END, L_F1, L_F2, L_I1, L_I2, L_C0, L_I3 = 0, 8, 16, 20, 24, 40, 48, 64, 72, 80
+
+
+def rank_program(g, core, T, topo):
+    rank = T.rank_of(core)
+    if rank is None:
+        return
+    Q = {"g": g, "v": g.vector, "s": g.scalar, "p": g.tensor, "y": g.sync}
+    cnt = {}
+    waited = {q: {} for q in Q}
+    log = {}
+
+    def A(name, a=0, b=None, st=1, rows=None):
+        t = T[name]
+        if b is None:
+            b = t.shape[1]
+        r = slice(None) if rows is None else rows
+        ap = t[r, a:b] if st == 1 else t[r, a:b:st]
+        if name in PSUM:
+            a, b = 0, 512
+        return (ap, [(name, a, b)])
+
+    def IND(win, off):
+        return (win[0].indirect(off[0]), win[1], off[1])
+
+    def L(c, n):
+        return A("LS", c, c + n)
+
+    def sync(q, reads, writes):
+        need = {}
+        for regs, wr in ((reads, False), (writes, True)):
+            for (nm, a, b) in regs:
+                for (lo, hi, eq, sem, v, ew) in log.get(nm, []):
+                    if hi <= a or b <= lo:
+                        continue
+                    if nm in PSUM:
+                        if eq == q and (q == "p" or not (wr or ew)):
+                            continue
+                    elif not (wr or ew):
+                        continue
+                    need[sem] = max(need.get(sem, 0), v)
+        for sem, v in need.items():
+            if waited[q].get(sem, 0) < v:
+                Q[q].wait_ge(T.sem[sem], v)
+                waited[q][sem] = v
+
+    def note(q, sem, v, reads, writes):
+        for (nm, a, b) in writes:
+            log[nm] = [e for e in log.get(nm, []) if not (a <= e[0] and e[1] <= b)] + [(a, b, q, sem, v, True)]
+        for (nm, a, b) in reads:
+            log[nm] = [e for e in log.get(nm, []) if not (not e[5] and e[3] == sem and a <= e[0] and e[1] <= b)] + [(a, b, q, sem, v, False)]
+
+    def run(q, fn, outs, ins):
+        reads, writes = [], []
+        for o in outs:
+            writes += o[1]
+            if len(o) == 3:
+                reads += o[2]
+        for i in ins:
+            if isinstance(i, tuple):
+                reads += i[1]
+                if len(i) == 3:
+                    reads += i[2]
+        sync(q, reads, writes)
+        sem = "q" + q
+        cnt[sem] = cnt.get(sem, 0) + 1
+        fn().then_inc(T.sem[sem], 1)
+        note(q, sem, cnt[sem], reads, writes)
+
+    def val(x):
+        return x[0] if isinstance(x, tuple) else x
+
+    def cp(o, i):
+        run("v", lambda: g.vector.tensor_copy(o[0], i[0]), [o], [i])
+
+    def tt(o, a, b, op):
+        run("v", lambda: g.vector.tensor_tensor(o[0], a[0], b[0], op), [o], [a, b])
+
+    def ts(o, a, s1, op0, s2=None, op1=None):
+        if op1 is None:
+            run("v", lambda: g.vector.tensor_scalar(o[0], a[0], val(s1), None, op0), [o], [a, s1])
+        else:
+            run("v", lambda: g.vector.tensor_scalar(o[0], a[0], val(s1), val(s2), op0, op1), [o], [a, s1, s2])
+
+    def scan(o, d0, d1, op0, op1):
+        run("v", lambda: g.vector.tensor_tensor_scan(o[0], d0[0], d1[0], 0.0, op0, op1), [o], [d0, d1])
+
+    def turn(o, i):
+        run("v", lambda: g.vector.transpose(o[0], i[0]), [o], [i])
+
+    def fill(o, c):
+        run("v", lambda: g.vector.memset(o[0], c), [o], [])
+
+    def act(o, i, f=AF.Identity, bias=0.0, scale=1.0):
+        run("s", lambda: g.scalar.activation(o[0], i[0], f, bias=val(bias), scale=val(scale)), [o], [i, bias, scale])
+
+    def mm(o, l, r, start=False, stop=False):
+        run("p", lambda: g.tensor.matmul(o[0], l[0], r[0], start, stop), [o], [l, r])
+
+    def iota(o, pat, base, cm, flt=False):
+        if flt:
+            run("g", lambda: g.iota(o[0], pat, base, cm, allow_small_or_imprecise_dtypes=True), [o], [])
+        else:
+            run("g", lambda: g.iota(o[0], pat, base, cm), [o], [])
+
+    def keep(o, pat, base, cm):
+        run("g", lambda: g.affine_select(o[0], o[0], pat, OP.is_ge, 0.0, base, cm), [o], [o])
+
+    def dma(q, sem, o, i):
+        sync(q, i[1], o[1])
+        Q[q].dma_start(o[0], i[0]).then_inc(T.sem[sem], 16)
+        cnt[sem] = 16
+        note("d", sem, 16, i[1], o[1])
+
+    def H(ap):
+        return (ap, [])
+
+    def send(dst_rank, o, i, sem):
+        dst = T.cores[dst_rank % N]
+        rid, pid, _ = topo.addr(dst)
+        sync("g", i[1], [])
+        g.remote_dma(o[0], i[0], T.sem[sem], T.sem["snt"], pid, rid, topo.mask(core, dst))
+        cnt["snt"] = cnt.get("snt", 0) + len(topo.engines(core, dst))
+
+    def lands(src_rank, o, sem):
+        n = len(topo.engines(T.cores[src_rank % N], core))
+        cnt[sem] = n
+        note("r", sem, n, [], o[1])
+
+    def partner_steps(t):
+        return A("PA%d" % t) if t < RO else A("W%d" % RO, 136, 200)
+
+    for t in range(1, RO + 1):
+        far = ((rank - 1) % N) ^ PX if t < RO else rank ^ PX
+        lands(far, partner_steps(t), "ap%d" % t)
+        lands(far, A("PZ%d" % t), "az%d" % t)
+        if t < RO:
+            lands(rank - 1, A("M%d" % t, 0, 224), "am%d" % t)
+            lands(rank - 1, A("W%d" % t, 16, 136), "ae%d" % t)
+
+    col = lambda j: A("CF", j, j + 1)
+    C_R, C_P7, C_P31, C_P, C_MSG, C_8R, C_DUM, C_RM, C_RM2, C_PG, C_A, C_F2, C_E1, C_E2 = range(14)
+    XW = A("X")
+    TOP = slice(0, 8)
+
+    dma("y", "dmem", A("mi"), H(T.mem[:]))
+    dma("s", "dnx", A("nxi"), H(T.nxt[:]))
+    dma("y", "dplc", A("pli", rows=TOP), H(T.plc[:]))
+    dma("s", "dz", A("M0", 96, 224), H(T.zt[:]))
+    dma("y", "dx1", A("X", 0, W), H(T.xt[:]))
+
+    iota(A("J1"), [[-1, 128]], 128, 1)
+    iota(A("J2"), [[-16, 8], [0, 16]], 128, 1)
+    iota(A("J3"), [[1, 144]], 0, 0)
+    iota(A("J4", rows=TOP), [[-1, 8], [0, 16]], 0, 1)
+    fill(A("ZR"), 0.0)
+    fill(A("KP"), 1.0)
+    for j in range(4):
+        fill(A("ZR", 4 + j, 256, 8), -32.0)
+    fill(A("KP", 0, 128, 16), 0.0)
+    fill(A("D0"), -129.0)
+    fill(A("C31"), 31.0)
+    fill(A("X", 2 * W, 2 * W + 384), 0.0)
+    keep(A("ZR"), [[-16, 8], [0, 32]], 0, 1)
+    keep(A("ZR"), [[16, 8], [0, 32]], 15, -1)
+    iota(A("IO", 0, W // 4), [[1, W // 4]], 0, 0, True)
+    ts(A("ta", 0, 128), A("J1"), 15, OP.bitwise_and)
+    ts(A("CI", 1, 2), A("J1", 0, 1), 7, OP.bitwise_and)
+    ts(A("CI", 2, 3), A("J1", 0, 1), 31, OP.bitwise_and)
+    ts(A("MK"), A("ta", 0, 128), 0.0, OP.is_equal)
+    ts(A("tb", 0, 128), A("J2"), 4, OP.arith_shift_right)
+    cp(col(C_R), A("ta", 0, 1))
+    ts(A("BO"), A("tb", 0, 128), 8.0, OP.is_equal)
+    cp(A("CF", 1, 3), A("CI", 1, 3))
+    ts(A("Ib"), A("J1"), 128.0, OP.is_equal)
+    for r in range(16):
+        ts(A("LP", 128 * r, 128 * r + 128), A("BO"), A("MK", r, r + 1), OP.mult)
+    act(col(C_MSG), col(C_P7), bias=15.0, scale=16.0)
+    act(col(C_A), col(C_R), bias=col(C_P31), scale=-0.875)
+    act(A("GS", 0, 8), A("BO", 0, 128, 16), scale=32.0)
+    act(col(C_F2), col(C_P7), bias=col(C_A), scale=31.875)
+    act(A("GS", 8, 16), A("BO", 0, 128, 16), scale=64.0)
+    act(A("GS", 16, 24), A("BO", 0, 128, 16), scale=-32.0)
+    act(A("GS", 24, 32), A("BO", 0, 128, 16), scale=8.0)
+    ts(A("tc"), A("J3", 0, 16), 1, OP.arith_shift_right)
+    ts(A("G8", rows=TOP), A("J4", rows=TOP), 0.0, OP.is_equal)
+    ts(L(L_F1, 16), A("tc"), 16.0, OP.mult, col(C_R), OP.add)
+    ts(L(L_F2, 8), A("J3", 0, 8), 2.0, OP.mult, col(C_F2), OP.add)
+    ts(L(L_C0, 8), A("J3", 0, 8), 0.0, OP.mult, col(C_MSG), OP.add)
+    ts(A("nxh"), A("nxi"), -2048.0, OP.add)
+    ts(A("ta", 0, 128), A("mi"), 1, OP.bitwise_and)
+    ts(A("plf", rows=TOP), A("pli", rows=TOP), 0.25, OP.add)
+    ts(A("fa", 0, 128), A("ta", 0, 128), -8193.0, OP.mult)
+    cp(A("M0", 224, 352), A("M0", 96, 224))
+    tt(A("fb", 0, 128), A("fa", 0, 128), A("mi"), OP.add)
+    cp(A("M0", 352, 608), A("M0", 96, 352))
+
+    banks = ["F1a", "F1b", "F2a", "F2b"]
+
+    def spread(b):
+        for h in range(2):
+            mm(A(banks[b % 4], 256 * h, 256 * h + 256), A("LP", 128 * (2 * b + h), 128 * (2 * b + h) + 128), A("nxh"), True, True)
+
+    def take(b):
+        act(A("NX", 512 * b, 512 * b + 512), A(banks[b % 4]), bias=2048.25)
+
+    spread(0)
+    mm(A("EX", 0, 128), A("G8", rows=TOP), A("plf", rows=TOP), True, True)
+    for b in range(1, 4):
+        spread(b)
+    for j in range(4):
+        mm(A("ZP", 128 * j, 128 * j + 128), A("Ib"), A("M0", 96, 224), True, True)
+    take(0)
+    take(1)
+
+    cp(A("fc"), IND(A("fb", 0, 128), L(L_F1, 16)))
+    tt(A("G1"), A("EX", 0, 128), A("MK"), OP.mult)
+    turn(A("fa"), A("fc"))
+    scan(A("G2"), A("KP"), A("G1"), OP.mult, OP.add)
+    act(A("W0", 8, 136), IND(A("fa"), L(L_F2, 8)), AF.Abs, bias=0.125, scale=0.5)
+    act(A("W0", 136, 264), A("W0", 8, 136), bias=float(W), scale=-1.0)
+    cp(L(L_REP, 8), A("J3", 0, 8))
+    cp(A("GS", 32, 40), A("J3", 0, 8))
+    ts(A("PN", 0, 4), A("J3", 0, 4), 2.0, OP.is_equal, 128.0, OP.mult)
+    fill(A("D0", 0, 256, 32), 1.0e6)
+    fill(A("D0", 16, 256, 32), 1919.0)
+    ts(L(L_MSG, 4), A("PN", 0, 4), col(C_MSG), OP.add)
+    for h in range(2):
+        tt(A("ta", 128 * h, 128 * h + 128), IND(A("G2"), L(L_C0, 8)), A("W0", 8 + 128 * h, 136 + 128 * h), OP.add)
+    take(2)
+    for h in range(2):
+        ts(A("tb", 128 * h, 128 * h + 128), A("ta", 128 * h, 128 * h + 128), W - 1, OP.bitwise_and)
+    for h in range(2):
+        cp(A("OFF", 128 * h, 128 * h + 128), A("tb", 128 * h, 128 * h + 128))
+    take(3)
+    act(A("W0", 0, 8), A("G2", 15, 128, 16))
+    for b in range(4, 8):
+        spread(b)
+
+    def late_columns():
+        act(col(C_RM), col(C_R), bias=-15.0 * STEP, scale=STEP)
+        act(col(C_RM2), col(C_R), bias=W - 15.0 * STEP, scale=STEP)
+        act(col(C_E1), col(C_P7), bias=2.0)
+        act(col(C_E2), col(C_P7), bias=8.0, scale=8.0)
+
+    def const(o, c, n):
+        iota(o, [[0, n]], int(c), 0, True)
+
+    def late_constants():
+        iota(A("DUM"), [[-16, 16]], -2 * W, -1, True)
+
+    def next_constants():
+        for t in range(1, RO):
+            const(A("W%d" % t, 8, 16), 0, 8)
+            const(A("W%d" % t, 136, 144), W, 8)
+            if t == 1:
+                const(A("WD"), 0, 144)
+                const(A("WD", 15, 144, 16), 1, 9)
+                keep(A("WD"), [[-1, 144]], 15, 1)
+                keep(A("WD"), [[1, 144]], 0, -1)
+
+    def next_lists():
+        ts(L(L_END, 1), col(C_E1), col(C_E2), OP.mult, -1.0, OP.add)
+        ts(L(L_TILE, 4), A("J3", 0, 4), 0.0, OP.mult, col(C_P7), OP.add)
+
+    def last_constants(t):
+        if t == 1:
+            act(col(C_8R), col(C_R), scale=8.0)
+            ts(L(L_I2, 8), A("J3", 0, 8), 32.0, OP.mult, col(C_P31), OP.add)
+            ts(col(C_A), col(C_R), 8.0, OP.is_ge, 64.0, OP.mult)
+        else:
+            ts(L(L_I1, 16), A("tc"), col(C_8R), OP.add)
+            ts(L(L_I3, 16), A("tc"), col(C_8R), OP.add, col(C_A), OP.add)
+
+    CA, CB = [0, 16, 8, 24], [4, 20, 12, 28]
+
+    def prepare(t):
+        Wt = "W%d" % t
+        act(A(Wt, 144, 200), A(Wt, 16, 72), bias=float(W), scale=-1.0)
+        mm(A("F1a", 0, 64), A("If"), A(Wt, 8, 72), True)
+        mm(A("F1b", 0, 64), A("If"), A(Wt, 136, 200), True)
+        mm(A("F2a", 0, 64), A("If"), A(Wt, 72, 136), True)
+        mm(A("F2b", 0, 64), A("nIf"), A(Wt, 72, 136), True)
+        tt(A("DIF"), A("PA%d" % t), A(Wt, 72, 136), OP.subtract)
+
+    def add_c(bank, M, stop=False):
+        for j in range(2):
+            mm(A(bank, 32 * j, 32 * j + 32), A("Ib"), A(M, 0, 32))
+            mm(A(bank, 32 * j, 32 * j + 32), A("Ib"), A(M, 48, 80), False, stop and j == 1)
+
+    def ex_diff(zo, t):
+        mm(A("EX", 0, 128), A("Ib"), zo, True)
+        mm(A("EX", 0, 128), A("nIb"), A("PZ%d" % t), False, True)
+
+    def ex_signs():
+        act(A("AB"), A("EX", 0, 128), AF.Abs)
+        act(A("S1"), A("AB"), AF.Sign, bias=LIM + 0.5, scale=-1.0)
+
+    def ex_count():
+        for r in range(16):
+            mm(A("EX", 128, 136), A("WD", 15 - r, 143 - r), A("S1", r, 128, 16), r == 0, r == 15)
+
+    def ex_alike():
+        act(A("SG"), A("EX", 128, 136), AF.Sign, bias=-1.0)
+        act(A("AL"), A("SG"), AF.Relu)
+
+    def ex_shift():
+        tt(A("TT"), IND(A("AL"), L(L_TILE, 4)), A("DIF"), OP.mult)
+
+    for t in range(RO):
+        Wt, M, O = "W%d" % t, "M%d" % t, "O%d" % t
+        last = t == RO - 1
+        Z, ZT = A(M, 96, 224), A(M, 96, 608)
+        XG = A("X", 0, W) if t == 0 else A("X", 0, 2 * W)
+
+        def gA(i):
+            tt(A("DA", 512 * i, 512 * i + 512), IND(XG, A("OFF", 8 * CA[i], 8 * CA[i] + 32)), ZT, OP.subtract)
+
+        def aA(i, lo=0, hi=4):
+            a, b = 512 * i + 128 * lo, 512 * i + 128 * hi
+            act(A("AD", a, b), A("DA", a, b), AF.Abs)
+
+        def gB(i):
+            act(A("XB", 512 * i, 512 * i + 512), IND(XG, A("OFF", 8 * CB[i], 8 * CB[i] + 32)), AF.Copy)
+
+        def mB(i, lo=0, hi=4):
+            a, b = 512 * i + 128 * lo, 512 * i + 128 * hi
+            tt(A("MB", a, b), A("XB", a, b), A("ZP", 0, b - a), OP.max)
+
+        def cost(buf, cs, i, k, stop=False, lo=0, hi=4):
+            for j in range(lo, hi):
+                mm(A("P", cs[i] + j, 256, 32), A(buf, 512 * i + 128 * j, 512 * i + 128 * j + 128), A("GS", 8 * k, 8 * k + 8), False, stop and j == 3)
+
+        def early():
+            if not last:
+                send(rank + 1, A("W%d" % (t + 1), 16, 136), A(Wt, 8, 128), "ae%d" % (t + 1))
+            send((rank ^ PX) + (0 if last else 1), partner_steps(t + 1), A(Wt, 64, 128), "ap%d" % (t + 1))
+
+        if t > 0:
+            for bank, ident in (("F1a", "Ib"), ("F1b", "nIb")):
+                mm(A(bank, 0, 8), A(ident), A(M, 32, 40))
+                mm(A(bank, 0, 8), A(ident), A(M, 80, 88))
+                add_c(bank, M, True)
+            for j in range(4):
+                mm(A("ZP", 128 * j, 128 * j + 128), A("Ib"), Z, True, True)
+            cp(A(M, 224, 352), Z)
+            cp(A(M, 352, 608), A(M, 96, 352))
+            cp(A("OFF", 0, 64), A("F1a", 0, 64))
+        else:
+            early()
+            const(A("DD"), -STEP, TRI[8])
+            iota(A("IO", W // 4, W), [[1, W - W // 4]], W // 4, 0, True)
+            late_constants()
+        mm(A("P", 0, 256), Z, A("ZR"), True)
+        mm(A("P", 0, 256), A("Ib"), A("C31"))
+        mm(A("WL", 0, 8), A("Ib"), A("GS", 32, 40), True)
+        gB(0)
+        gA(0)
+        if t == 0:
+            dma("y", "dx2", A("X", W, 2 * W), (T.xt[:], [("X", 0, 1)]))
+        if t > 0:
+            ex_diff(Z, t)
+            cp(A("OFF", 128, 192), A("F1b", 0, 64))
+            ex_signs()
+            add_c("F2a", M)
+            add_c("F2b", M)
+            ex_count()
+        cost("XB", CB, 0, 2)
+        gB(1)
+        gA(1)
+        if t > 0:
+            ex_alike()
+        mB(0)
+        aA(0)
+        cost("XB", CB, 1, 2)
+        if t > 0:
+            ex_shift()
+            mm(A("F2a", 0, 64), A("If"), A("TT"), False, True)
+            mm(A("F2b", 0, 64), A("nIf"), A("TT"), False, True)
+            tt(A(Wt, 0, 16), A(M, 24, 40), A(M, 72, 88), OP.add)
+            tt(A(Wt, 72, 136), A(Wt, 72, 136), A("TT"), OP.add)
+            early()
+        mB(1)
+        cost("MB", CB, 0, 1)
+        cost("AD", CA, 0, 0)
+        aA(1)
+        if t > 0:
+            cp(A("OFF", 64, 128), A("F2a", 0, 64))
+            ts(A("OFF", 192, 256), A("F2b", 0, 64), float(W), OP.add)
+        cost("MB", CB, 1, 1)
+        cost("AD", CA, 1, 0)
+        gB(2)
+        gA(2)
+        cost("XB", CB, 2, 2)
+        gB(3)
+        gA(3)
+        aA(2)
+        mB(2)
+        cost("XB", CB, 3, 2)
+        cost("AD", CA, 2, 0)
+        cost("MB", CB, 2, 1)
+        for lo, hi in ((0, 2), (2, 3), (3, 4)):
+            aA(3, lo, hi)
+            mB(3, lo, hi)
+            cost("AD", CA, 3, 0, False, lo, hi)
+            cost("MB", CB, 3, 1, hi == 4, lo, hi)
+        if t > 0:
+            act(A(Wt, 136, 144), A(Wt, 8, 16), bias=float(W), scale=-1.0)
+            act(A(Wt, 200, 264), A(Wt, 72, 136), bias=float(W), scale=-1.0)
+            act(A("ZM"), Z, bias=-192.0)
+        else:
+            for b in range(4, 8):
+                take(b)
+        if last:
+            act(A("W%d" % RO, 16, 136), A(Wt, 8, 128))
+
+        def reset(*segments):
+            if t == 0:
+                for s in segments:
+                    fill(A("DD", TRI[s], TRI[s] + 1), 2 * FAR)
+
+        scan(A("SC"), A("D0"), A("P", 0, 256), OP.add, OP.min)
+        reset(0)
+        ts(A("IDX"), A("SC", 31, 256, 32), 31, OP.bitwise_and)
+        reset(1)
+        tt(A("LT"), IND(A("IDX"), L(L_REP, 8)), A("MK"), OP.mult)
+        mm(A("WL", 0, 8), A("LT"), A("GS", 24, 32), False, True)
+        reset(2, 3)
+        cp(A("WO"), A("WL", 0, 8))
+        reset(4)
+        tt(A("G1"), IND(A(Wt, 8, 264), A("WO")), A("MK"), OP.mult)
+        reset(5)
+        scan(A("SS", 128, 256), A("KP"), A("G1"), OP.mult, OP.add)
+        reset(6)
+        tt(A("Q1"), A("SS", 143, 256, 16), A(Wt, 0, 8), OP.add)
+        reset(7)
+        ts(A("Q2"), A("Q1"), W - 1, OP.bitwise_and)
+        cp(A("QO"), A("Q2"))
+
+        def walk():
+            for o, w in ((("XQ", "X"), ("QN", "IO")) if not last else (("QN", "IO"), ("XQ", "X"))):
+                act(A(o), IND(A(w, 0, W), A("QO")), AF.Copy)
+
+        def newz():
+            tt(A("DQ"), A("XQ"), A("ZP", 0, 128), OP.subtract)
+            act(A(O, 96, 224), A("DQ"), AF.Abs)
+
+        def search(by_scalar, which=(7, 6, 5, 4, 3, 2, 1, 0)):
+            for s in which:
+                o, i = A("E", TRI[s], TRI[s + 1]), A("QN", 0, 16 * s + 16)
+                if s in by_scalar:
+                    act(o, i, AF.Abs, bias=A("NB", s, s + 1), scale=FAR)
+                else:
+                    ts(o, i, A("QF", s, s + 1), OP.not_equal, FAR, OP.mult)
+            if 0 in which:
+                act(A("QR", 0, 8), A("QF"), bias=col(C_RM))
+                act(A("QR", 8, 16), A("QF"), bias=col(C_RM2))
+                act(A("T1"), A("DQ"), bias=191.75, scale=0.5)
+
+        def update(between):
+            scan(A("ES"), A("DD"), A("E"), OP.add, OP.min)
+            between[0]()
+            tt(A("LO"), IND(A("ES"), L(L_END, 1)), A("QR"), OP.subtract)
+            between[1]()
+            tt(A("LO2"), A("LO"), A("DUM"), OP.max)
+            between[2]()
+            ts(A("SO"), A("LO2"), -1.0, OP.mult)
+            between[3]()
+            tt(IND(XW, A("SO", 0, 8)), A("T1"), A("ZM"), OP.add)
+            if not last:
+                tt(IND(XW, A("SO", 8, 16)), A("T1"), A("ZM"), OP.add)
+
+        if not last:
+            walk()
+            tt(A("G2"), IND(A("NX"), A("QO")), A("MK"), OP.mult)
+            newz()
+            scan(A("SS", 0, 128), A("KP"), A("G2"), OP.mult, OP.add)
+            cp(A("QF"), A("Q2"))
+            cp(A(O, 0, 48), IND(A("SS"), L(L_MSG, 3)))
+            tt(A(O, 48, 96), IND(A("SS"), L(L_MSG, 3)), A(O, 0, 48), OP.subtract)
+            send(rank + 1, A("M%d" % (t + 1), 0, 224), A(O), "am%d" % (t + 1))
+            send((rank ^ PX) + 1, A("PZ%d" % (t + 1)), A(O, 96, 224), "az%d" % (t + 1))
+            act(A("NB"), A("QF"), scale=-FAR)
+            if t == 0:
+                next_constants()
+                late_columns()
+                search((2,))
+                next_lists()
+                act(A("ZM"), Z, bias=-192.0)
+                act(A("If"), A("Ib"))
+            else:
+                search((6, 5, 2))
+            act(A("H8"), A("WL", 0, 8), AF.Sign, bias=-127.5)
+            if t == 0:
+                act(A("nIf"), A("Ib"), scale=-1.0)
+                act(A("nIb"), A("Ib"), scale=-1.0)
+            for j in range(8):
+                mm(A("WL", 8, 9), A("C31", 0, 128), A("H8", j, j + 1), j == 0, j == 7)
+            update([lambda: ts(A("PI", 0, 1), A("WL", 8, 9), 16.0 / 31.0, OP.mult, 16384.25, OP.add),
+                    lambda: ts(A("PI", 4, 5), A("PI", 0, 1), 1023, OP.bitwise_and),
+                    lambda: ts(A("PN", 0, 1), A("PI", 4, 5), -1.0, OP.mult, 1919.0, OP.add),
+                    lambda: prepare(t + 1)])
+            act(A("D0", 16, 256, 32), A("QF"), bias=A("PN", 0, 1), scale=0.0)
+            if t > 0:
+                last_constants(t)
+        else:
+            WF = "W%d" % RO
+            walk()
+            cp(A("QF"), A("Q2"))
+            ts(A("NB"), A("Q2"), -FAR, OP.mult)
+            search((), (7, 6))
+            newz()
+            send(rank ^ PX, A("PZ%d" % RO), A(O, 96, 224), "az%d" % RO)
+            search((4,), (5, 4, 3, 2, 1, 0))
+            update([lambda: None] * 4)
+            dma("y", "dyx", H(T.yx[:]), A("X", 0, W))
+            act(A(WF, 8, 16), A("SS", 143, 256, 16))
+            act(A("YC"), IND(A("NX"), A("QO")), bias=-0.25)
+            dma("s", "dyz", H(T.yz[:]), A(O, 96, 224))
+            dma("s", "dyc", H(T.yc[:]), A("YC", rows=slice(0, 128, 16)))
+            ts(A("ta", 0, 192), A(WF, 8, 200), 0.25, OP.add)
+            tt(A("fa", 0, 192), A(WF, 8, 200), A("ta", 0, 192), OP.is_lt)
+            ts(A("fb", 0, 192), A("fa", 0, 192), -4096.25, OP.mult)
+            tt(A("U"), A("fb", 0, 192), A(WF, 8, 200), OP.add)
+            cp(A("fc"), IND(A("U"), L(L_I1, 16)))
+            turn(A("fa"), A("fc"))
+            cp(A("fc"), IND(A("U"), L(L_I3, 16)))
+            turn(A("fb"), A("fc"))
+            act(A("G1"), IND(A("fa"), L(L_I2, 8)), AF.Abs, bias=-0.25, scale=2.0)
+            ex_diff(A(O, 96, 224), RO)
+            ex_signs()
+            act(A("G2"), IND(A("fb"), L(L_I2, 8)), AF.Abs, bias=-0.25, scale=2.0)
+            mm(A("EX", 128, 256), A("BO"), A("S1"), True, True)
+            ts(A("F1a", 0, 128), A("EX", 128, 256), 1.0, OP.is_ge)
+            tt(A("SS", 0, 128), A("G2"), A("G1"), OP.subtract)
+            tt(A("F1b", 0, 128), A("SS", 0, 128), A("F1a", 0, 128), OP.mult)
+            tt(A("YH"), A("G1"), A("F1b", 0, 128), OP.add)
+            dma("y", "dyh", H(T.yh[:]), A("YH"))
+
+    for sem, n in cnt.items():
+        g.wait_ge(T.sem[sem], n)

@@ -27,9 +27,10 @@ SCRATCH = {
     "SC": ("sbuf", [128, 256], "int32"), "C31": ("sbuf", [128, 256], "bfloat16"), "IDX": ("sbuf", [128, 8], "int32"),
     "LT": ("sbuf", [128, 128], "bfloat16"), "WO": ("sbuf", [128, 8], "uint16"),
     "G1": ("sbuf", [128, 128], "float32"), "G2": ("sbuf", [128, 128], "float32"), "SS": ("sbuf", [128, 256], "float32"),
-    "Q1": ("sbuf", [128, 8], "int32"), "Q2": ("sbuf", [128, 8], "int32"), "QO": ("sbuf", [128, 8], "uint16"),
-    "XQ": ("sbuf", [128, 128], "bfloat16"), "DQ": ("sbuf", [128, 128], "bfloat16"),
-    "T1": ("sbuf", [128, 128], "bfloat16"), "ZM": ("sbuf", [128, 128], "bfloat16"),
+    "Q1": ("sbuf", [128, 128], "int32"), "Q2": ("sbuf", [128, 8], "int32"), "QO": ("sbuf", [128, 8], "uint16"),
+    "XQ": ("sbuf", [128, 128], "bfloat16"), "PL": ("sbuf", [128, 256], "float32"),
+    "T1": ("sbuf", [128, 256], "bfloat16"), "ZM": ("sbuf", [128, 256], "bfloat16"),
+    "SUM": ("sbuf", [128, 64], "float32"), "MID": ("sbuf", [128, 64], "float32"), "HD": ("sbuf", [128, 64], "float32"),
     "QN": ("sbuf", [128, 128], "float32"), "QF": ("sbuf", [128, 8], "float32"), "NB": ("sbuf", [128, 8], "float32"),
     "QR": ("sbuf", [128, 16], "float32"),
     "E": ("sbuf", [128, 576], "bfloat16"), "ES": ("sbuf", [128, 576], "bfloat16"),
@@ -37,7 +38,7 @@ SCRATCH = {
     "H8": ("sbuf", [128, 8], "bfloat16"), "PN": ("sbuf", [128, 8], "float32"), "PI": ("sbuf", [128, 8], "int32"),
     "DIF": ("sbuf", [128, 64], "float32"), "TT": ("sbuf", [128, 64], "float32"),
     "AB": ("sbuf", [128, 128], "bfloat16"), "S1": ("sbuf", [128, 128], "bfloat16"),
-    "SG": ("sbuf", [128, 8], "float32"), "AL": ("sbuf", [128, 8], "float32"),
+    "SG": ("sbuf", [128, 8], "float32"),
     "YC": ("sbuf", [128, 128], "float32"), "YH": ("sbuf", [128, 128], "float32"), "U": ("sbuf", [128, 192], "float32"),
 }
 for _t in range(RO + 1):
@@ -65,7 +66,7 @@ def rank_program(g, core, T, topo):
     Q = {"g": g, "v": g.vector, "s": g.scalar, "p": g.tensor, "y": g.sync}
     cnt = {}
     waited = {q: {} for q in Q}
-    log = {}
+    log, order, known = {}, {}, {}
 
     def A(name, a=0, b=None, st=1, rows=None):
         t = T[name]
@@ -96,12 +97,17 @@ def rank_program(g, core, T, topo):
                     elif not (wr or ew):
                         continue
                     need[sem] = max(need.get(sem, 0), v)
-        for sem, v in need.items():
+        for sem, v in sorted(need.items(), key=lambda e: -order.get(e, 0)):
             if waited[q].get(sem, 0) < v:
                 Q[q].wait_ge(T.sem[sem], v)
                 waited[q][sem] = v
+                for s2, v2 in known.get((sem, v), {}).items():
+                    waited[q][s2] = max(waited[q].get(s2, 0), v2)
 
     def note(q, sem, v, reads, writes):
+        order[(sem, v)] = len(order) + 1
+        if q in waited:
+            known[(sem, v)] = dict(waited[q])
         for (nm, a, b) in writes:
             log[nm] = [e for e in log.get(nm, []) if not (a <= e[0] and e[1] <= b)] + [(a, b, q, sem, v, True)]
         for (nm, a, b) in reads:
@@ -210,28 +216,32 @@ def rank_program(g, core, T, topo):
     iota(A("J2"), [[-16, 8], [0, 16]], 128, 1)
     iota(A("J3"), [[1, 144]], 0, 0)
     iota(A("J4", rows=TOP), [[-1, 8], [0, 16]], 0, 1)
-    fill(A("ZR"), 0.0)
-    fill(A("KP"), 1.0)
-    for j in range(4):
-        fill(A("ZR", 4 + j, 256, 8), -32.0)
-    fill(A("KP", 0, 128, 16), 0.0)
-    fill(A("D0"), -129.0)
+    iota(A("ZR"), [[0, 32], [-32, 2], [0, 4]], 0, 0, True)
     fill(A("C31"), 31.0)
+    fill(A("KP"), 1.0)
     fill(A("X", 2 * W, 2 * W + 384), 0.0)
+    fill(A("KP", 0, 128, 16), 0.0)
+    act(A("D0"), A("C31"), bias=-129.0, scale=0.0)
+    act(A("D0", 0, 256, 32), A("C31", 0, 8), bias=1.0e6, scale=0.0)
+    act(A("D0", 16, 256, 32), A("C31", 0, 8), bias=1919.0, scale=0.0)
     keep(A("ZR"), [[-16, 8], [0, 32]], 0, 1)
     keep(A("ZR"), [[16, 8], [0, 32]], 15, -1)
     iota(A("IO", 0, W // 4), [[1, W // 4]], 0, 0, True)
     ts(A("ta", 0, 128), A("J1"), 15, OP.bitwise_and)
     ts(A("CI", 1, 2), A("J1", 0, 1), 7, OP.bitwise_and)
     ts(A("CI", 2, 3), A("J1", 0, 1), 31, OP.bitwise_and)
+    ts(A("Ib"), A("J1"), 128.0, OP.is_equal)
     ts(A("MK"), A("ta", 0, 128), 0.0, OP.is_equal)
     ts(A("tb", 0, 128), A("J2"), 4, OP.arith_shift_right)
     cp(col(C_R), A("ta", 0, 1))
-    ts(A("BO"), A("tb", 0, 128), 8.0, OP.is_equal)
     cp(A("CF", 1, 3), A("CI", 1, 3))
-    ts(A("Ib"), A("J1"), 128.0, OP.is_equal)
-    for r in range(16):
-        ts(A("LP", 128 * r, 128 * r + 128), A("BO"), A("MK", r, r + 1), OP.mult)
+    ts(A("tc"), A("J3", 0, 16), 1, OP.arith_shift_right)
+    cp(L(L_REP, 8), A("J3", 0, 8))
+    ts(A("BO"), A("tb", 0, 128), 8.0, OP.is_equal)
+    cp(A("GS", 32, 40), A("J3", 0, 8))
+    ts(A("PN", 0, 4), A("J3", 0, 4), 2.0, OP.is_equal, 128.0, OP.mult)
+    ts(L(L_F1, 16), A("tc"), 16.0, OP.mult, col(C_R), OP.add)
+    ts(A("G8", rows=TOP), A("J4", rows=TOP), 0.0, OP.is_equal)
     act(col(C_MSG), col(C_P7), bias=15.0, scale=16.0)
     act(col(C_A), col(C_R), bias=col(C_P31), scale=-0.875)
     act(A("GS", 0, 8), A("BO", 0, 128, 16), scale=32.0)
@@ -239,18 +249,24 @@ def rank_program(g, core, T, topo):
     act(A("GS", 8, 16), A("BO", 0, 128, 16), scale=64.0)
     act(A("GS", 16, 24), A("BO", 0, 128, 16), scale=-32.0)
     act(A("GS", 24, 32), A("BO", 0, 128, 16), scale=8.0)
-    ts(A("tc"), A("J3", 0, 16), 1, OP.arith_shift_right)
-    ts(A("G8", rows=TOP), A("J4", rows=TOP), 0.0, OP.is_equal)
-    ts(L(L_F1, 16), A("tc"), 16.0, OP.mult, col(C_R), OP.add)
+
+
+    def pick(*rs):
+        for r in rs:
+            ts(A("LP", 128 * r, 128 * r + 128), A("BO"), A("MK", r, r + 1), OP.mult)
+
+    pick(*range(8))
+    act(A("nIb"), A("Ib"), scale=-1.0)
+    ts(A("ta", 0, 128), A("mi"), 1, OP.bitwise_and)
+    ts(A("nxh"), A("nxi"), -2048.0, OP.add)
+    ts(A("fa", 0, 128), A("ta", 0, 128), -8193.0, OP.mult)
+    ts(A("plf", rows=TOP), A("pli", rows=TOP), 0.25, OP.add)
     ts(L(L_F2, 8), A("J3", 0, 8), 2.0, OP.mult, col(C_F2), OP.add)
     ts(L(L_C0, 8), A("J3", 0, 8), 0.0, OP.mult, col(C_MSG), OP.add)
-    ts(A("nxh"), A("nxi"), -2048.0, OP.add)
-    ts(A("ta", 0, 128), A("mi"), 1, OP.bitwise_and)
-    ts(A("plf", rows=TOP), A("pli", rows=TOP), 0.25, OP.add)
-    ts(A("fa", 0, 128), A("ta", 0, 128), -8193.0, OP.mult)
-    cp(A("M0", 224, 352), A("M0", 96, 224))
     tt(A("fb", 0, 128), A("fa", 0, 128), A("mi"), OP.add)
-    cp(A("M0", 352, 608), A("M0", 96, 352))
+    cp(A("M0", 224, 352), A("M0", 96, 224))
+    ts(L(L_MSG, 4), A("PN", 0, 4), col(C_MSG), OP.add)
+    pick(8, 9)
 
     banks = ["F1a", "F1b", "F2a", "F2b"]
 
@@ -272,16 +288,13 @@ def rank_program(g, core, T, topo):
 
     cp(A("fc"), IND(A("fb", 0, 128), L(L_F1, 16)))
     tt(A("G1"), A("EX", 0, 128), A("MK"), OP.mult)
+    cp(A("M0", 352, 608), A("M0", 96, 352))
     turn(A("fa"), A("fc"))
     scan(A("G2"), A("KP"), A("G1"), OP.mult, OP.add)
     act(A("W0", 8, 136), IND(A("fa"), L(L_F2, 8)), AF.Abs, bias=0.125, scale=0.5)
+    act(A("W0", 0, 8), A("G2", 15, 128, 16))
     act(A("W0", 136, 264), A("W0", 8, 136), bias=float(W), scale=-1.0)
-    cp(L(L_REP, 8), A("J3", 0, 8))
-    cp(A("GS", 32, 40), A("J3", 0, 8))
-    ts(A("PN", 0, 4), A("J3", 0, 4), 2.0, OP.is_equal, 128.0, OP.mult)
-    fill(A("D0", 0, 256, 32), 1.0e6)
-    fill(A("D0", 16, 256, 32), 1919.0)
-    ts(L(L_MSG, 4), A("PN", 0, 4), col(C_MSG), OP.add)
+    pick(*range(10, 16))
     for h in range(2):
         tt(A("ta", 128 * h, 128 * h + 128), IND(A("G2"), L(L_C0, 8)), A("W0", 8 + 128 * h, 136 + 128 * h), OP.add)
     take(2)
@@ -290,7 +303,6 @@ def rank_program(g, core, T, topo):
     for h in range(2):
         cp(A("OFF", 128 * h, 128 * h + 128), A("tb", 128 * h, 128 * h + 128))
     take(3)
-    act(A("W0", 0, 8), A("G2", 15, 128, 16))
     for b in range(4, 8):
         spread(b)
 
@@ -309,7 +321,6 @@ def rank_program(g, core, T, topo):
     def next_constants():
         for t in range(1, RO):
             const(A("W%d" % t, 8, 16), 0, 8)
-            const(A("W%d" % t, 136, 144), W, 8)
             if t == 1:
                 const(A("WD"), 0, 144)
                 const(A("WD", 15, 144, 16), 1, 9)
@@ -333,12 +344,12 @@ def rank_program(g, core, T, topo):
 
     def prepare(t):
         Wt = "W%d" % t
-        act(A(Wt, 144, 200), A(Wt, 16, 72), bias=float(W), scale=-1.0)
+        act(A("MID"), A("SUM"), scale=0.5)
+        act(A("HD"), A("DIF"), scale=0.5)
         mm(A("F1a", 0, 64), A("If"), A(Wt, 8, 72), True)
-        mm(A("F1b", 0, 64), A("If"), A(Wt, 136, 200), True)
-        mm(A("F2a", 0, 64), A("If"), A(Wt, 72, 136), True)
-        mm(A("F2b", 0, 64), A("nIf"), A(Wt, 72, 136), True)
-        tt(A("DIF"), A("PA%d" % t), A(Wt, 72, 136), OP.subtract)
+        mm(A("F1b", 0, 64), A("nIf"), A(Wt, 8, 72), True)
+        mm(A("F2a", 0, 64), A("If"), A("MID"), True)
+        mm(A("F2b", 0, 64), A("nIf"), A("MID"), True)
 
     def add_c(bank, M, stop=False):
         for j in range(2):
@@ -349,8 +360,9 @@ def rank_program(g, core, T, topo):
         mm(A("EX", 0, 128), A("Ib"), zo, True)
         mm(A("EX", 0, 128), A("nIb"), A("PZ%d" % t), False, True)
 
-    def ex_signs():
+    def ex_signs(between):
         act(A("AB"), A("EX", 0, 128), AF.Abs)
+        between()
         act(A("S1"), A("AB"), AF.Sign, bias=LIM + 0.5, scale=-1.0)
 
     def ex_count():
@@ -359,10 +371,9 @@ def rank_program(g, core, T, topo):
 
     def ex_alike():
         act(A("SG"), A("EX", 128, 136), AF.Sign, bias=-1.0)
-        act(A("AL"), A("SG"), AF.Relu)
 
     def ex_shift():
-        tt(A("TT"), IND(A("AL"), L(L_TILE, 4)), A("DIF"), OP.mult)
+        tt(A("TT"), IND(A("SG"), L(L_TILE, 4)), A("HD"), OP.mult)
 
     for t in range(RO):
         Wt, M, O = "W%d" % t, "M%d" % t, "O%d" % t
@@ -393,6 +404,10 @@ def rank_program(g, core, T, topo):
                 send(rank + 1, A("W%d" % (t + 1), 16, 136), A(Wt, 8, 128), "ae%d" % (t + 1))
             send((rank ^ PX) + (0 if last else 1), partner_steps(t + 1), A(Wt, 64, 128), "ap%d" % (t + 1))
 
+        def lower():
+            for h in range(1 if last else 2):
+                act(A("ZM", 128 * h, 128 * h + 128), Z, bias=-192.0)
+
         if t > 0:
             for bank, ident in (("F1a", "Ib"), ("F1b", "nIb")):
                 mm(A(bank, 0, 8), A(ident), A(M, 32, 40))
@@ -400,9 +415,11 @@ def rank_program(g, core, T, topo):
                 add_c(bank, M, True)
             for j in range(4):
                 mm(A("ZP", 128 * j, 128 * j + 128), A("Ib"), Z, True, True)
-            cp(A(M, 224, 352), Z)
-            cp(A(M, 352, 608), A(M, 96, 352))
+            for j in range(3):
+                cp(A(M, 224 + 128 * j, 352 + 128 * j), Z)
+            tt(A(Wt, 0, 16), A(M, 24, 40), A(M, 72, 88), OP.add)
             cp(A("OFF", 0, 64), A("F1a", 0, 64))
+            ts(A("OFF", 128, 192), A("F1b", 0, 64), float(W), OP.add)
         else:
             early()
             const(A("DD"), -STEP, TRI[8])
@@ -417,8 +434,7 @@ def rank_program(g, core, T, topo):
             dma("y", "dx2", A("X", W, 2 * W), (T.xt[:], [("X", 0, 1)]))
         if t > 0:
             ex_diff(Z, t)
-            cp(A("OFF", 128, 192), A("F1b", 0, 64))
-            ex_signs()
+            ex_signs(lower)
             add_c("F2a", M)
             add_c("F2b", M)
             ex_count()
@@ -434,14 +450,13 @@ def rank_program(g, core, T, topo):
             ex_shift()
             mm(A("F2a", 0, 64), A("If"), A("TT"), False, True)
             mm(A("F2b", 0, 64), A("nIf"), A("TT"), False, True)
-            tt(A(Wt, 0, 16), A(M, 24, 40), A(M, 72, 88), OP.add)
-            tt(A(Wt, 72, 136), A(Wt, 72, 136), A("TT"), OP.add)
-            early()
         mB(1)
         cost("MB", CB, 0, 1)
         cost("AD", CA, 0, 0)
         aA(1)
         if t > 0:
+            tt(A(Wt, 72, 136), A("MID"), A("TT"), OP.add)
+            early()
             cp(A("OFF", 64, 128), A("F2a", 0, 64))
             ts(A("OFF", 192, 256), A("F2b", 0, 64), float(W), OP.add)
         cost("MB", CB, 1, 1)
@@ -462,14 +477,18 @@ def rank_program(g, core, T, topo):
             cost("AD", CA, 3, 0, False, lo, hi)
             cost("MB", CB, 3, 1, hi == 4, lo, hi)
         if t > 0:
-            act(A(Wt, 136, 144), A(Wt, 8, 16), bias=float(W), scale=-1.0)
-            act(A(Wt, 200, 264), A(Wt, 72, 136), bias=float(W), scale=-1.0)
-            act(A("ZM"), Z, bias=-192.0)
+            for j, bank in enumerate(("F1a", "F2a", "F1b", "F2b")):
+                act(A("PL", 64 * j, 64 * j + 64), A(bank, 0, 64), bias=float(W) if j > 1 else 0.0)
         else:
+            late_columns()
             for b in range(4, 8):
                 take(b)
         if last:
             act(A("W%d" % RO, 16, 136), A(Wt, 8, 128))
+
+        def both_steps():
+            tt(A("SUM"), A("PA%d" % (t + 1)), A("W%d" % (t + 1), 72, 136), OP.add)
+            tt(A("DIF"), A("PA%d" % (t + 1)), A("W%d" % (t + 1), 72, 136), OP.subtract)
 
         def reset(*segments):
             if t == 0:
@@ -477,42 +496,62 @@ def rank_program(g, core, T, topo):
                     fill(A("DD", TRI[s], TRI[s] + 1), 2 * FAR)
 
         scan(A("SC"), A("D0"), A("P", 0, 256), OP.add, OP.min)
-        reset(0)
+        reset(0, 1)
         ts(A("IDX"), A("SC", 31, 256, 32), 31, OP.bitwise_and)
-        reset(1)
+        reset(2, 3)
         tt(A("LT"), IND(A("IDX"), L(L_REP, 8)), A("MK"), OP.mult)
         mm(A("WL", 0, 8), A("LT"), A("GS", 24, 32), False, True)
-        reset(2, 3)
+        reset(4, 5, 6, 7)
+        if 0 < t < RO - 1:
+            last_constants(t)
         cp(A("WO"), A("WL", 0, 8))
-        reset(4)
-        tt(A("G1"), IND(A(Wt, 8, 264), A("WO")), A("MK"), OP.mult)
-        reset(5)
-        scan(A("SS", 128, 256), A("KP"), A("G1"), OP.mult, OP.add)
-        reset(6)
-        tt(A("Q1"), A("SS", 143, 256, 16), A(Wt, 0, 8), OP.add)
-        reset(7)
-        ts(A("Q2"), A("Q1"), W - 1, OP.bitwise_and)
+
+
+        def reversals():
+            act(A("H8"), A("WL", 0, 8), AF.Sign, bias=-127.5)
+            for j in range(8):
+                mm(A("WL", 8, 9), A("C31", 0, 128), A("H8", j, j + 1), j == 0, j == 7)
+
+        if 0 < t < RO - 1:
+            reversals()
+        if t == 0:
+            next_lists()
+            tt(A("G1"), IND(A(Wt, 8, 264), A("WO")), A("MK"), OP.mult)
+            scan(A("SS", 128, 256), A("KP"), A("G1"), OP.mult, OP.add)
+            tt(A("Q1", 0, 8), A("SS", 143, 256, 16), A(Wt, 0, 8), OP.add)
+            ts(A("Q2"), A("Q1", 0, 8), W - 1, OP.bitwise_and)
+        else:
+            tt(A("G1"), IND(A("PL"), A("WO")), A("MK"), OP.mult)
+            scan(A("Q1"), A("KP"), A("G1"), OP.mult, OP.add)
+            scan(A("G2"), A("KP"), A("G1"), OP.mult, OP.add)
+            ts(A("Q2"), A("Q1", 15, 128, 16), W - 1, OP.bitwise_and)
+            tt(A("W%d" % RO, 8, 16) if last else A("SS", 143, 256, 16), A("G2", 15, 128, 16), A(Wt, 0, 8), OP.subtract)
         cp(A("QO"), A("Q2"))
+        ts(A("NB"), A("Q2"), -FAR, OP.mult)
 
         def walk():
-            for o, w in ((("XQ", "X"), ("QN", "IO")) if not last else (("QN", "IO"), ("XQ", "X"))):
+            for o, w in (("QN", "IO"), ("XQ", "X")):
                 act(A(o), IND(A(w, 0, W), A("QO")), AF.Copy)
 
-        def newz():
-            tt(A("DQ"), A("XQ"), A("ZP", 0, 128), OP.subtract)
-            act(A(O, 96, 224), A("DQ"), AF.Abs)
+        def marks():
+            ts(A("QR", 0, 8), A("Q2"), col(C_RM), OP.add)
+            ts(A("QR", 8, 16), A("Q2"), col(C_RM2), OP.add)
 
-        def search(by_scalar, which=(7, 6, 5, 4, 3, 2, 1, 0)):
+        def newz():
+            mm(A("EX", 0, 128), A("nIb"), Z, True)
+            mm(A("EX", 0, 128), A("Ib"), A("XQ"), False, True)
+            search("s", 4, 3, 1, 0)
+            act(A(O, 96, 224), A("EX", 0, 128), AF.Abs)
+            for h in range(1 if last else 2):
+                act(A("T1", 128 * h, 128 * h + 128), A("EX", 0, 128), bias=191.75, scale=0.5)
+
+        def search(q, *which):
             for s in which:
                 o, i = A("E", TRI[s], TRI[s + 1]), A("QN", 0, 16 * s + 16)
-                if s in by_scalar:
+                if q == "s":
                     act(o, i, AF.Abs, bias=A("NB", s, s + 1), scale=FAR)
                 else:
                     ts(o, i, A("QF", s, s + 1), OP.not_equal, FAR, OP.mult)
-            if 0 in which:
-                act(A("QR", 0, 8), A("QF"), bias=col(C_RM))
-                act(A("QR", 8, 16), A("QF"), bias=col(C_RM2))
-                act(A("T1"), A("DQ"), bias=191.75, scale=0.5)
 
         def update(between):
             scan(A("ES"), A("DD"), A("E"), OP.add, OP.min)
@@ -523,73 +562,63 @@ def rank_program(g, core, T, topo):
             between[2]()
             ts(A("SO"), A("LO2"), -1.0, OP.mult)
             between[3]()
-            tt(IND(XW, A("SO", 0, 8)), A("T1"), A("ZM"), OP.add)
-            if not last:
-                tt(IND(XW, A("SO", 8, 16)), A("T1"), A("ZM"), OP.add)
+            n = 8 if last else 16
+            tt(IND(XW, A("SO", 0, n)), A("T1", 0, 16 * n), A("ZM", 0, 16 * n), OP.add)
 
         if not last:
             walk()
             tt(A("G2"), IND(A("NX"), A("QO")), A("MK"), OP.mult)
             newz()
-            scan(A("SS", 0, 128), A("KP"), A("G2"), OP.mult, OP.add)
             cp(A("QF"), A("Q2"))
+            scan(A("SS", 0, 128), A("KP"), A("G2"), OP.mult, OP.add)
+            search("v", 7)
             cp(A(O, 0, 48), IND(A("SS"), L(L_MSG, 3)))
+            search("v", 6)
             tt(A(O, 48, 96), IND(A("SS"), L(L_MSG, 3)), A(O, 0, 48), OP.subtract)
             send(rank + 1, A("M%d" % (t + 1), 0, 224), A(O), "am%d" % (t + 1))
             send((rank ^ PX) + 1, A("PZ%d" % (t + 1)), A(O, 96, 224), "az%d" % (t + 1))
-            act(A("NB"), A("QF"), scale=-FAR)
+            search("v", 5, 2)
+            marks()
             if t == 0:
                 next_constants()
-                late_columns()
-                search((2,))
-                next_lists()
-                act(A("ZM"), Z, bias=-192.0)
+                reversals()
+                lower()
                 act(A("If"), A("Ib"))
-            else:
-                search((6, 5, 2))
-            act(A("H8"), A("WL", 0, 8), AF.Sign, bias=-127.5)
-            if t == 0:
                 act(A("nIf"), A("Ib"), scale=-1.0)
-                act(A("nIb"), A("Ib"), scale=-1.0)
-            for j in range(8):
-                mm(A("WL", 8, 9), A("C31", 0, 128), A("H8", j, j + 1), j == 0, j == 7)
-            update([lambda: ts(A("PI", 0, 1), A("WL", 8, 9), 16.0 / 31.0, OP.mult, 16384.25, OP.add),
+            update([both_steps,
+                    lambda: (prepare(t + 1), ts(A("PI", 0, 1), A("WL", 8, 9), 16.0 / 31.0, OP.mult, 16384.25, OP.add)),
                     lambda: ts(A("PI", 4, 5), A("PI", 0, 1), 1023, OP.bitwise_and),
-                    lambda: ts(A("PN", 0, 1), A("PI", 4, 5), -1.0, OP.mult, 1919.0, OP.add),
-                    lambda: prepare(t + 1)])
+                    lambda: ts(A("PN", 0, 1), A("PI", 4, 5), -1.0, OP.mult, 1919.0, OP.add)])
             act(A("D0", 16, 256, 32), A("QF"), bias=A("PN", 0, 1), scale=0.0)
-            if t > 0:
-                last_constants(t)
         else:
             WF = "W%d" % RO
             walk()
             cp(A("QF"), A("Q2"))
-            ts(A("NB"), A("Q2"), -FAR, OP.mult)
-            search((), (7, 6))
+            marks()
+            ts(A("ta", 0, 192), A(WF, 8, 200), 0.25, OP.add)
             newz()
             send(rank ^ PX, A("PZ%d" % RO), A(O, 96, 224), "az%d" % RO)
-            search((4,), (5, 4, 3, 2, 1, 0))
-            update([lambda: None] * 4)
+            search("v", 7, 6, 5, 2)
+            update([lambda: tt(A("fa", 0, 128), A(WF, 8, 136), A("ta", 0, 128), OP.is_lt),
+                    lambda: (tt(A("fa", 128, 192), A(WF, 136, 200), A("ta", 128, 192), OP.is_lt),
+                             ts(A("fb", 0, 128), A("fa", 0, 128), -4096.25, OP.mult)),
+                    lambda: tt(A("U", 0, 128), A("fb", 0, 128), A(WF, 8, 136), OP.add),
+                    lambda: ts(A("fb", 128, 192), A("fa", 128, 192), -4096.25, OP.mult)])
             dma("y", "dyx", H(T.yx[:]), A("X", 0, W))
-            act(A(WF, 8, 16), A("SS", 143, 256, 16))
             act(A("YC"), IND(A("NX"), A("QO")), bias=-0.25)
-            dma("s", "dyz", H(T.yz[:]), A(O, 96, 224))
-            dma("s", "dyc", H(T.yc[:]), A("YC", rows=slice(0, 128, 16)))
-            ts(A("ta", 0, 192), A(WF, 8, 200), 0.25, OP.add)
-            tt(A("fa", 0, 192), A(WF, 8, 200), A("ta", 0, 192), OP.is_lt)
-            ts(A("fb", 0, 192), A("fa", 0, 192), -4096.25, OP.mult)
-            tt(A("U"), A("fb", 0, 192), A(WF, 8, 200), OP.add)
-            cp(A("fc"), IND(A("U"), L(L_I1, 16)))
+            dma("y", "dyz", H(T.yz[:]), A(O, 96, 224))
+            dma("y", "dyc", H(T.yc[:]), A("YC", rows=slice(0, 128, 16)))
+            tt(A("U", 128, 192), A("fb", 128, 192), A(WF, 136, 200), OP.add)
+            cp(A("fc"), IND(A("U", 0, 128), L(L_I1, 16)))
+            act(A("PL"), IND(A("U"), L(L_I3, 16)), AF.Copy)
             turn(A("fa"), A("fc"))
-            cp(A("fc"), IND(A("U"), L(L_I3, 16)))
-            turn(A("fb"), A("fc"))
-            act(A("G1"), IND(A("fa"), L(L_I2, 8)), AF.Abs, bias=-0.25, scale=2.0)
+            turn(A("fb"), A("PL"))
             ex_diff(A(O, 96, 224), RO)
-            ex_signs()
-            act(A("G2"), IND(A("fb"), L(L_I2, 8)), AF.Abs, bias=-0.25, scale=2.0)
+            act(A("G1"), IND(A("fa"), L(L_I2, 8)), AF.Abs, bias=-0.25, scale=2.0)
+            ex_signs(lambda: act(A("G2"), IND(A("fb"), L(L_I2, 8)), AF.Abs, bias=-0.25, scale=2.0))
             mm(A("EX", 128, 256), A("BO"), A("S1"), True, True)
-            ts(A("F1a", 0, 128), A("EX", 128, 256), 1.0, OP.is_ge)
             tt(A("SS", 0, 128), A("G2"), A("G1"), OP.subtract)
+            ts(A("F1a", 0, 128), A("EX", 128, 256), 1.0, OP.is_ge)
             tt(A("F1b", 0, 128), A("SS", 0, 128), A("F1a", 0, 128), OP.mult)
             tt(A("YH"), A("G1"), A("F1b", 0, 128), OP.add)
             dma("y", "dyh", H(T.yh[:]), A("YH"))

from concourse.mybir import AluOpType as OP, ActivationFunctionType as AF

N, W, RO, PX, LIM = 8, 4096, 4, 2, 11
TRI = [8 * s * (s + 1) for s in range(9)]
STEP, FAR = 16384.0, 4194304.0

SCRATCH = {
    "X": ("sbuf", [128, 2 * W + 384], "bfloat16"),
    "NX": ("sbuf", [128, W], "float32"), "IO": ("sbuf", [128, W], "float32"),
    "nxi": ("sbuf", [128, 256], "int32"), "nxh": ("sbuf", [128, 256], "float16"),
    "LP": ("sbuf", [128, 2048], "float16"),
    "mi": ("sbuf", [128, 128], "int32"), "pli": ("sbuf", [128, 128], "int32"), "plf": ("sbuf", [128, 128], "float32"),
    "J1": ("sbuf", [128, 128], "int32"), "J2": ("sbuf", [128, 128], "int32"), "J3": ("sbuf", [128, 144], "int32"),
    "J4": ("sbuf", [128, 128], "int32"), "G8": ("sbuf", [128, 128], "float32"),
    "ta": ("sbuf", [128, 256], "int32"), "tb": ("sbuf", [128, 256], "int32"), "tc": ("sbuf", [128, 16], "int32"),
    "fa": ("sbuf", [128, 256], "float32"), "fb": ("sbuf", [128, 256], "float32"), "fc": ("sbuf", [128, 256], "float32"),
    "CI": ("sbuf", [128, 8], "int32"), "CF": ("sbuf", [128, 24], "float32"),
    "Ib": ("sbuf", [128, 128], "bfloat16"), "nIb": ("sbuf", [128, 128], "bfloat16"),
    "If": ("sbuf", [128, 128], "float32"), "nIf": ("sbuf", [128, 128], "float32"),
    "MK": ("sbuf", [128, 128], "bfloat16"), "KP": ("sbuf", [128, 128], "bfloat16"),
    "BO": ("sbuf", [128, 128], "bfloat16"), "ZR": ("sbuf", [128, 256], "bfloat16"), "GS": ("sbuf", [128, 40], "bfloat16"),
    "WD": ("sbuf", [128, 144], "bfloat16"),
    "D0": ("sbuf", [128, 256], "float32"), "DD": ("sbuf", [128, 576], "bfloat16"), "DUM": ("sbuf", [128, 16], "float32"),
    "LS": ("sbuf", [128, 96], "uint16"), "OFF": ("sbuf", [128, 256], "uint16"),
    "DA": ("sbuf", [128, 2048], "bfloat16"), "AD": ("sbuf", [128, 2048], "bfloat16"),
    "XB": ("sbuf", [128, 2048], "bfloat16"), "MB": ("sbuf", [128, 2048], "bfloat16"),
    "SC": ("sbuf", [128, 256], "int32"), "C31": ("sbuf", [128, 256], "bfloat16"), "IDX": ("sbuf", [128, 8], "int32"),
    "LT": ("sbuf", [128, 128], "bfloat16"), "WO": ("sbuf", [128, 8], "uint16"),
    "G1": ("sbuf", [128, 128], "float32"), "G2": ("sbuf", [128, 128], "float32"), "SS": ("sbuf", [128, 256], "float32"),
    "Q1": ("sbuf", [128, 128], "int32"), "Q2": ("sbuf", [128, 8], "int32"), "QO": ("sbuf", [128, 8], "uint16"),
    "XQ": ("sbuf", [128, 128], "bfloat16"), "PL": ("sbuf", [128, 256], "float32"),
    "T1": ("sbuf", [128, 256], "bfloat16"), "ZM": ("sbuf", [128, 256], "bfloat16"),
    "SUM": ("sbuf", [128, 64], "float32"), "MID": ("sbuf", [128, 64], "float32"), "HD": ("sbuf", [128, 64], "float32"),
    "QN": ("sbuf", [128, 128], "float32"), "QF": ("sbuf", [128, 8], "float32"), "NB": ("sbuf", [128, 8], "float32"),
    "QR": ("sbuf", [128, 16], "float32"),
    "E": ("sbuf", [128, 576], "bfloat16"), "ES": ("sbuf", [128, 576], "bfloat16"),
    "LO": ("sbuf", [128, 16], "float32"), "LO2": ("sbuf", [128, 16], "float32"), "SO": ("sbuf", [128, 16], "uint16"),
    "H8": ("sbuf", [128, 8], "bfloat16"), "PN": ("sbuf", [128, 8], "float32"), "PI": ("sbuf", [128, 8], "int32"),
    "DIF": ("sbuf", [128, 64], "float32"), "TT": ("sbuf", [128, 64], "float32"),
    "AB": ("sbuf", [128, 128], "bfloat16"), "S1": ("sbuf", [128, 128], "bfloat16"),
    "SG": ("sbuf", [128, 8], "float32"),
    "YC": ("sbuf", [128, 128], "float32"), "YH": ("sbuf", [128, 128], "float32"), "U": ("sbuf", [128, 192], "float32"),
}
for _t in range(RO + 1):
    SCRATCH["W%d" % _t] = ("sbuf", [128, 264], "float32")
    if _t > 0:
        SCRATCH["PA%d" % _t] = ("sbuf", [128, 64], "float32")
        SCRATCH["PZ%d" % _t] = ("sbuf", [128, 128], "bfloat16")
    if _t < RO:
        SCRATCH["M%d" % _t] = ("sbuf", [128, 608], "bfloat16")
        SCRATCH["O%d" % _t] = ("sbuf", [128, 224], "bfloat16")
PSUM = ["P", "ZP", "F1a", "F1b", "F2a", "F2b", "EX", "WL"]
for _n in PSUM:
    SCRATCH[_n] = ("psum", [128, 512], "float32")

DMAS = ["dmem", "dplc", "dz", "dnx", "dx1", "dx2", "dyz", "dyc", "dyx", "dyh"]
SEMAPHORES = ["qv", "qs", "qp", "qg", "snt"] + DMAS + [k + str(t) for t in range(1, RO + 1) for k in ("am", "az", "ae", "ap")]

L_TILE, L_REP, L_MSG, L_END, L_F1, L_F2, L_I1, L_I2, L_C0, L_I3 = 0, 8, 16, 20, 24, 40, 48, 64, 72, 80


def rank_program(g, core, T, topo):
    rank = T.rank_of(core)
    if rank is None:
        return
    Q = {"g": g, "v": g.vector, "s": g.scalar, "p": g.tensor, "y": g.sync}
    cnt = {}
    waited = {q: {} for q in Q}
    log, order, known = {}, {}, {}

    def A(name, a=0, b=None, st=1, rows=None):
        t = T[name]
        if b is None:
            b = t.shape[1]
        r = slice(None) if rows is None else rows
        ap = t[r, a:b] if st == 1 else t[r, a:b:st]
        if name in PSUM:
            a, b = 0, 512
        return (ap, [(name, a, b)])

    def IND(win, off):
        return (win[0].indirect(off[0]), win[1], off[1])

    def L(c, n):
        return A("LS", c, c + n)

    def sync(q, reads, writes):
        need = {}
        for regs, wr in ((reads, False), (writes, True)):
            for (nm, a, b) in regs:
                for (lo, hi, eq, sem, v, ew) in log.get(nm, []):
                    if hi <= a or b <= lo:
                        continue
                    if nm in PSUM:
                        if eq == q and (q == "p" or not (wr or ew)):
                            continue
                    elif not (wr or ew):
                        continue
                    need[sem] = max(need.get(sem, 0), v)
        for sem, v in sorted(need.items(), key=lambda e: -order.get(e, 0)):
            if waited[q].get(sem, 0) < v:
                Q[q].wait_ge(T.sem[sem], v)
                waited[q][sem] = v
                for s2, v2 in known.get((sem, v), {}).items():
                    waited[q][s2] = max(waited[q].get(s2, 0), v2)

    def note(q, sem, v, reads, writes):
        order[(sem, v)] = len(order) + 1
        if q in waited:
            known[(sem, v)] = dict(waited[q])
        for (nm, a, b) in writes:
            log[nm] = [e for e in log.get(nm, []) if not (a <= e[0] and e[1] <= b)] + [(a, b, q, sem, v, True)]
        for (nm, a, b) in reads:
            log[nm] = [e for e in log.get(nm, []) if not (not e[5] and e[3] == sem and a <= e[0] and e[1] <= b)] + [(a, b, q, sem, v, False)]

    def run(q, fn, outs, ins):
        reads, writes = [], []
        for o in outs:
            writes += o[1]
            if len(o) == 3:
                reads += o[2]
        for i in ins:
            if isinstance(i, tuple):
                reads += i[1]
                if len(i) == 3:
                    reads += i[2]
        sync(q, reads, writes)
        sem = "q" + q
        cnt[sem] = cnt.get(sem, 0) + 1
        fn().then_inc(T.sem[sem], 1)
        note(q, sem, cnt[sem], reads, writes)

    def val(x):
        return x[0] if isinstance(x, tuple) else x

    def cp(o, i):
        run("v", lambda: g.vector.tensor_copy(o[0], i[0]), [o], [i])

    def tt(o, a, b, op):
        run("v", lambda: g.vector.tensor_tensor(o[0], a[0], b[0], op), [o], [a, b])

    def ts(o, a, s1, op0, s2=None, op1=None):
        if op1 is None:
            run("v", lambda: g.vector.tensor_scalar(o[0], a[0], val(s1), None, op0), [o], [a, s1])
        else:
            run("v", lambda: g.vector.tensor_scalar(o[0], a[0], val(s1), val(s2), op0, op1), [o], [a, s1, s2])

    def scan(o, d0, d1, op0, op1):
        run("v", lambda: g.vector.tensor_tensor_scan(o[0], d0[0], d1[0], 0.0, op0, op1), [o], [d0, d1])

    def turn(o, i):
        run("v", lambda: g.vector.transpose(o[0], i[0]), [o], [i])

    def fill(o, c):
        run("v", lambda: g.vector.memset(o[0], c), [o], [])

    def act(o, i, f=AF.Identity, bias=0.0, scale=1.0):
        run("s", lambda: g.scalar.activation(o[0], i[0], f, bias=val(bias), scale=val(scale)), [o], [i, bias, scale])

    def mm(o, l, r, start=False, stop=False):
        run("p", lambda: g.tensor.matmul(o[0], l[0], r[0], start, stop), [o], [l, r])

    def iota(o, pat, base, cm, flt=False):
        if flt:
            run("g", lambda: g.iota(o[0], pat, base, cm, allow_small_or_imprecise_dtypes=True), [o], [])
        else:
            run("g", lambda: g.iota(o[0], pat, base, cm), [o], [])

    def keep(o, pat, base, cm):
        run("g", lambda: g.affine_select(o[0], o[0], pat, OP.is_ge, 0.0, base, cm), [o], [o])

    def dma(q, sem, o, i):
        sync(q, i[1], o[1])
        Q[q].dma_start(o[0], i[0]).then_inc(T.sem[sem], 16)
        cnt[sem] = 16
        note("d", sem, 16, i[1], o[1])

    def H(ap):
        return (ap, [])

    def send(dst_rank, o, i, sem):
        dst = T.cores[dst_rank % N]
        rid, pid, _ = topo.addr(dst)
        sync("g", i[1], [])
        g.remote_dma(o[0], i[0], T.sem[sem], T.sem["snt"], pid, rid, topo.mask(core, dst))
        cnt["snt"] = cnt.get("snt", 0) + len(topo.engines(core, dst))

    def lands(src_rank, o, sem):
        n = len(topo.engines(T.cores[src_rank % N], core))
        cnt[sem] = n
        note("r", sem, n, [], o[1])

    def partner_steps(t):
        return A("PA%d" % t) if t < RO else A("W%d" % RO, 136, 200)

    for t in range(1, RO + 1):
        far = ((rank - 1) % N) ^ PX if t < RO else rank ^ PX
        lands(far, partner_steps(t), "ap%d" % t)
        lands(far, A("PZ%d" % t), "az%d" % t)
        if t < RO:
            lands(rank - 1, A("M%d" % t, 0, 224), "am%d" % t)
            lands(rank - 1, A("W%d" % t, 16, 136), "ae%d" % t)

    col = lambda j: A("CF", j, j + 1)
    C_R, C_P7, C_P31, C_P, C_MSG, C_8R, C_DUM, C_RM, C_RM2, C_PG, C_A, C_F2, C_E1, C_E2 = range(14)
    XW = A("X")
    TOP = slice(0, 8)

    dma("y", "dmem", A("mi"), H(T.mem[:]))
    dma("s", "dnx", A("nxi"), H(T.nxt[:]))
    dma("y", "dplc", A("pli", rows=TOP), H(T.plc[:]))
    dma("s", "dz", A("M0", 96, 224), H(T.zt[:]))
    dma("y", "dx1", A("X", 0, W), H(T.xt[:]))

    iota(A("J1"), [[-1, 128]], 128, 1)
    iota(A("J2"), [[-16, 8], [0, 16]], 128, 1)
    iota(A("J3"), [[1, 144]], 0, 0)
    iota(A("J4", rows=TOP), [[-1, 8], [0, 16]], 0, 1)
    iota(A("ZR"), [[0, 32], [-32, 2], [0, 4]], 0, 0, True)
    fill(A("C31"), 31.0)
    fill(A("KP"), 1.0)
    fill(A("X", 2 * W, 2 * W + 384), 0.0)
    fill(A("KP", 0, 128, 16), 0.0)
    act(A("D0"), A("C31"), bias=-129.0, scale=0.0)
    act(A("D0", 0, 256, 32), A("C31", 0, 8), bias=1.0e6, scale=0.0)
    act(A("D0", 16, 256, 32), A("C31", 0, 8), bias=1919.0, scale=0.0)
    keep(A("ZR"), [[-16, 8], [0, 32]], 0, 1)
    keep(A("ZR"), [[16, 8], [0, 32]], 15, -1)
    iota(A("IO", 0, W // 4), [[1, W // 4]], 0, 0, True)
    ts(A("ta", 0, 128), A("J1"), 15, OP.bitwise_and)
    ts(A("CI", 1, 2), A("J1", 0, 1), 7, OP.bitwise_and)
    ts(A("CI", 2, 3), A("J1", 0, 1), 31, OP.bitwise_and)
    ts(A("Ib"), A("J1"), 128.0, OP.is_equal)
    ts(A("MK"), A("ta", 0, 128), 0.0, OP.is_equal)
    ts(A("tb", 0, 128), A("J2"), 4, OP.arith_shift_right)
    cp(col(C_R), A("ta", 0, 1))
    cp(A("CF", 1, 3), A("CI", 1, 3))
    ts(A("tc"), A("J3", 0, 16), 1, OP.arith_shift_right)
    cp(L(L_REP, 8), A("J3", 0, 8))
    ts(A("BO"), A("tb", 0, 128), 8.0, OP.is_equal)
    cp(A("GS", 32, 40), A("J3", 0, 8))
    ts(A("PN", 0, 4), A("J3", 0, 4), 2.0, OP.is_equal, 128.0, OP.mult)
    ts(L(L_F1, 16), A("tc"), 16.0, OP.mult, col(C_R), OP.add)
    ts(A("G8", rows=TOP), A("J4", rows=TOP), 0.0, OP.is_equal)
    act(col(C_MSG), col(C_P7), bias=15.0, scale=16.0)
    act(col(C_A), col(C_R), bias=col(C_P31), scale=-0.875)
    act(A("GS", 0, 8), A("BO", 0, 128, 16), scale=32.0)
    act(col(C_F2), col(C_P7), bias=col(C_A), scale=31.875)
    act(A("GS", 8, 16), A("BO", 0, 128, 16), scale=64.0)
    act(A("GS", 16, 24), A("BO", 0, 128, 16), scale=-32.0)
    act(A("GS", 24, 32), A("BO", 0, 128, 16), scale=8.0)


    def pick(*rs):
        for r in rs:
            ts(A("LP", 128 * r, 128 * r + 128), A("BO"), A("MK", r, r + 1), OP.mult)

    pick(*range(8))
    act(A("nIb"), A("Ib"), scale=-1.0)
    ts(A("ta", 0, 128), A("mi"), 1, OP.bitwise_and)
    ts(A("nxh"), A("nxi"), -2048.0, OP.add)
    ts(A("fa", 0, 128), A("ta", 0, 128), -8193.0, OP.mult)
    ts(A("plf", rows=TOP), A("pli", rows=TOP), 0.25, OP.add)
    ts(L(L_F2, 8), A("J3", 0, 8), 2.0, OP.mult, col(C_F2), OP.add)
    ts(L(L_C0, 8), A("J3", 0, 8), 0.0, OP.mult, col(C_MSG), OP.add)
    tt(A("fb", 0, 128), A("fa", 0, 128), A("mi"), OP.add)
    cp(A("M0", 224, 352), A("M0", 96, 224))
    ts(L(L_MSG, 4), A("PN", 0, 4), col(C_MSG), OP.add)
    pick(8, 9)

    banks = ["F1a", "F1b", "F2a", "F2b"]

    def spread(b):
        for h in range(2):
            mm(A(banks[b % 4], 256 * h, 256 * h + 256), A("LP", 128 * (2 * b + h), 128 * (2 * b + h) + 128), A("nxh"), True, True)

    def take(b):
        act(A("NX", 512 * b, 512 * b + 512), A(banks[b % 4]), bias=2048.25)

    spread(0)
    mm(A("EX", 0, 128), A("G8", rows=TOP), A("plf", rows=TOP), True, True)
    for b in range(1, 4):
        spread(b)
    for j in range(4):
        mm(A("ZP", 128 * j, 128 * j + 128), A("Ib"), A("M0", 96, 224), True, True)
    take(0)
    take(1)

    cp(A("fc"), IND(A("fb", 0, 128), L(L_F1, 16)))
    tt(A("G1"), A("EX", 0, 128), A("MK"), OP.mult)
    cp(A("M0", 352, 608), A("M0", 96, 352))
    turn(A("fa"), A("fc"))
    scan(A("G2"), A("KP"), A("G1"), OP.mult, OP.add)
    act(A("W0", 8, 136), IND(A("fa"), L(L_F2, 8)), AF.Abs, bias=0.125, scale=0.5)
    act(A("W0", 0, 8), A("G2", 15, 128, 16))
    act(A("W0", 136, 264), A("W0", 8, 136), bias=float(W), scale=-1.0)
    pick(*range(10, 16))
    for h in range(2):
        tt(A("ta", 128 * h, 128 * h + 128), IND(A("G2"), L(L_C0, 8)), A("W0", 8 + 128 * h, 136 + 128 * h), OP.add)
    take(2)
    for h in range(2):
        ts(A("tb", 128 * h, 128 * h + 128), A("ta", 128 * h, 128 * h + 128), W - 1, OP.bitwise_and)
    for h in range(2):
        cp(A("OFF", 128 * h, 128 * h + 128), A("tb", 128 * h, 128 * h + 128))
    take(3)
    for b in range(4, 8):
        spread(b)

    def late_columns():
        act(col(C_RM), col(C_R), bias=-15.0 * STEP, scale=STEP)
        act(col(C_RM2), col(C_R), bias=W - 15.0 * STEP, scale=STEP)
        act(col(C_E1), col(C_P7), bias=2.0)
        act(col(C_E2), col(C_P7), bias=8.0, scale=8.0)

    def const(o, c, n):
        iota(o, [[0, n]], int(c), 0, True)

    def late_constants():
        iota(A("DUM"), [[-16, 16]], -2 * W, -1, True)

    def next_constants():
        for t in range(1, RO):
            const(A("W%d" % t, 8, 16), 0, 8)
            if t == 1:
                const(A("WD"), 0, 144)
                const(A("WD", 15, 144, 16), 1, 9)
                keep(A("WD"), [[-1, 144]], 15, 1)
                keep(A("WD"), [[1, 144]], 0, -1)

    def next_lists():
        ts(L(L_END, 1), col(C_E1), col(C_E2), OP.mult, -1.0, OP.add)
        ts(L(L_TILE, 4), A("J3", 0, 4), 0.0, OP.mult, col(C_P7), OP.add)

    def last_constants(t):
        if t == 1:
            act(col(C_8R), col(C_R), scale=8.0)
            ts(L(L_I2, 8), A("J3", 0, 8), 32.0, OP.mult, col(C_P31), OP.add)
            ts(col(C_A), col(C_R), 8.0, OP.is_ge, 64.0, OP.mult)
        else:
            ts(L(L_I1, 16), A("tc"), col(C_8R), OP.add)
            ts(L(L_I3, 16), A("tc"), col(C_8R), OP.add, col(C_A), OP.add)

    CA, CB = [0, 16, 8, 24], [4, 20, 12, 28]

    def prepare(t):
        Wt = "W%d" % t
        act(A("MID"), A("SUM"), scale=0.5)
        act(A("HD"), A("DIF"), scale=0.5)
        mm(A("F1a", 0, 64), A("If"), A(Wt, 8, 72), True)
        mm(A("F1b", 0, 64), A("nIf"), A(Wt, 8, 72), True)
        mm(A("F2a", 0, 64), A("If"), A("MID"), True)
        mm(A("F2b", 0, 64), A("nIf"), A("MID"), True)

    def add_c(bank, M, stop=False):
        for j in range(2):
            mm(A(bank, 32 * j, 32 * j + 32), A("Ib"), A(M, 0, 32))
            mm(A(bank, 32 * j, 32 * j + 32), A("Ib"), A(M, 48, 80), False, stop and j == 1)

    def ex_diff(zo, t):
        mm(A("EX", 0, 128), A("Ib"), zo, True)
        mm(A("EX", 0, 128), A("nIb"), A("PZ%d" % t), False, True)

    def ex_signs(between):
        act(A("AB"), A("EX", 0, 128), AF.Abs)
        between()
        act(A("S1"), A("AB"), AF.Sign, bias=LIM + 0.5, scale=-1.0)

    def ex_count():
        for r in range(16):
            mm(A("EX", 128, 136), A("WD", 15 - r, 143 - r), A("S1", r, 128, 16), r == 0, r == 15)

    def ex_alike():
        act(A("SG"), A("EX", 128, 136), AF.Sign, bias=-1.0)

    def ex_shift():
        tt(A("TT"), IND(A("SG"), L(L_TILE, 4)), A("HD"), OP.mult)

    for t in range(RO):
        Wt, M, O = "W%d" % t, "M%d" % t, "O%d" % t
        last = t == RO - 1
        Z, ZT = A(M, 96, 224), A(M, 96, 608)
        XG = A("X", 0, W) if t == 0 else A("X", 0, 2 * W)

        def gA(i):
            tt(A("DA", 512 * i, 512 * i + 512), IND(XG, A("OFF", 8 * CA[i], 8 * CA[i] + 32)), ZT, OP.subtract)

        def aA(i, lo=0, hi=4):
            a, b = 512 * i + 128 * lo, 512 * i + 128 * hi
            act(A("AD", a, b), A("DA", a, b), AF.Abs)

        def gB(i):
            act(A("XB", 512 * i, 512 * i + 512), IND(XG, A("OFF", 8 * CB[i], 8 * CB[i] + 32)), AF.Copy)

        def mB(i, lo=0, hi=4):
            a, b = 512 * i + 128 * lo, 512 * i + 128 * hi
            tt(A("MB", a, b), A("XB", a, b), A("ZP", 0, b - a), OP.max)

        def cost(buf, cs, i, k, stop=False, lo=0, hi=4):
            for j in range(lo, hi):
                mm(A("P", cs[i] + j, 256, 32), A(buf, 512 * i + 128 * j, 512 * i + 128 * j + 128), A("GS", 8 * k, 8 * k + 8), False, stop and j == 3)

        def early():
            if not last:
                send(rank + 1, A("W%d" % (t + 1), 16, 136), A(Wt, 8, 128), "ae%d" % (t + 1))
            send((rank ^ PX) + (0 if last else 1), partner_steps(t + 1), A(Wt, 64, 128), "ap%d" % (t + 1))

        def lower():
            for h in range(1 if last else 2):
                act(A("ZM", 128 * h, 128 * h + 128), Z, bias=-192.0)

        if t > 0:
            for bank, ident in (("F1a", "Ib"), ("F1b", "nIb")):
                mm(A(bank, 0, 8), A(ident), A(M, 32, 40))
                mm(A(bank, 0, 8), A(ident), A(M, 80, 88))
                add_c(bank, M, True)
            for j in range(4):
                mm(A("ZP", 128 * j, 128 * j + 128), A("Ib"), Z, True, True)
            for j in range(3):
                cp(A(M, 224 + 128 * j, 352 + 128 * j), Z)
            tt(A(Wt, 0, 16), A(M, 24, 40), A(M, 72, 88), OP.add)
            cp(A("OFF", 0, 64), A("F1a", 0, 64))
            ts(A("OFF", 128, 192), A("F1b", 0, 64), float(W), OP.add)
        else:
            early()
            const(A("DD"), -STEP, TRI[8])
            iota(A("IO", W // 4, W), [[1, W - W // 4]], W // 4, 0, True)
            late_constants()
        mm(A("P", 0, 256), Z, A("ZR"), True)
        mm(A("P", 0, 256), A("Ib"), A("C31"))
        mm(A("WL", 0, 8), A("Ib"), A("GS", 32, 40), True)
        gB(0)
        gA(0)
        if t == 0:
            dma("y", "dx2", A("X", W, 2 * W), (T.xt[:], [("X", 0, 1)]))
        if t > 0:
            ex_diff(Z, t)
            ex_signs(lower)
            add_c("F2a", M)
            add_c("F2b", M)
            ex_count()
        cost("XB", CB, 0, 2)
        gB(1)
        gA(1)
        if t > 0:
            ex_alike()
        mB(0)
        aA(0)
        cost("XB", CB, 1, 2)
        if t > 0:
            ex_shift()
            mm(A("F2a", 0, 64), A("If"), A("TT"), False, True)
            mm(A("F2b", 0, 64), A("nIf"), A("TT"), False, True)
        mB(1)
        cost("MB", CB, 0, 1)
        cost("AD", CA, 0, 0)
        aA(1)
        if t > 0:
            tt(A(Wt, 72, 136), A("MID"), A("TT"), OP.add)
            early()
            cp(A("OFF", 64, 128), A("F2a", 0, 64))
            ts(A("OFF", 192, 256), A("F2b", 0, 64), float(W), OP.add)
        cost("MB", CB, 1, 1)
        cost("AD", CA, 1, 0)
        gB(2)
        gA(2)
        cost("XB", CB, 2, 2)
        gB(3)
        gA(3)
        aA(2)
        mB(2)
        cost("XB", CB, 3, 2)
        cost("AD", CA, 2, 0)
        cost("MB", CB, 2, 1)
        for lo, hi in ((0, 2), (2, 3), (3, 4)):
            aA(3, lo, hi)
            mB(3, lo, hi)
            cost("AD", CA, 3, 0, False, lo, hi)
            cost("MB", CB, 3, 1, hi == 4, lo, hi)
        if t > 0:
            for j, bank in enumerate(("F1a", "F2a", "F1b", "F2b")):
                act(A("PL", 64 * j, 64 * j + 64), A(bank, 0, 64), bias=float(W) if j > 1 else 0.0)
        else:
            late_columns()
            for b in range(4, 8):
                take(b)
        if last:
            act(A("W%d" % RO, 16, 136), A(Wt, 8, 128))

        def both_steps():
            tt(A("SUM"), A("PA%d" % (t + 1)), A("W%d" % (t + 1), 72, 136), OP.add)
            tt(A("DIF"), A("PA%d" % (t + 1)), A("W%d" % (t + 1), 72, 136), OP.subtract)

        def reset(*segments):
            if t == 0:
                for s in segments:
                    fill(A("DD", TRI[s], TRI[s] + 1), 2 * FAR)

        scan(A("SC"), A("D0"), A("P", 0, 256), OP.add, OP.min)
        reset(0, 1)
        ts(A("IDX"), A("SC", 31, 256, 32), 31, OP.bitwise_and)
        reset(2, 3)
        tt(A("LT"), IND(A("IDX"), L(L_REP, 8)), A("MK"), OP.mult)
        mm(A("WL", 0, 8), A("LT"), A("GS", 24, 32), False, True)
        reset(4, 5, 6, 7)
        if 0 < t < RO - 1:
            last_constants(t)
        cp(A("WO"), A("WL", 0, 8))


        def reversals():
            act(A("H8"), A("WL", 0, 8), AF.Sign, bias=-127.5)
            for j in range(8):
                mm(A("WL", 8, 9), A("C31", 0, 128), A("H8", j, j + 1), j == 0, j == 7)

        if 0 < t < RO - 1:
            reversals()
        if t == 0:
            next_lists()
            tt(A("G1"), IND(A(Wt, 8, 264), A("WO")), A("MK"), OP.mult)
            scan(A("SS", 128, 256), A("KP"), A("G1"), OP.mult, OP.add)
            tt(A("Q1", 0, 8), A("SS", 143, 256, 16), A(Wt, 0, 8), OP.add)
            ts(A("Q2"), A("Q1", 0, 8), W - 1, OP.bitwise_and)
        else:
            tt(A("G1"), IND(A("PL"), A("WO")), A("MK"), OP.mult)
            scan(A("Q1"), A("KP"), A("G1"), OP.mult, OP.add)
            scan(A("G2"), A("KP"), A("G1"), OP.mult, OP.add)
            ts(A("Q2"), A("Q1", 15, 128, 16), W - 1, OP.bitwise_and)
            tt(A("W%d" % RO, 8, 16) if last else A("SS", 143, 256, 16), A("G2", 15, 128, 16), A(Wt, 0, 8), OP.subtract)
        cp(A("QO"), A("Q2"))
        ts(A("NB"), A("Q2"), -FAR, OP.mult)

        def walk():
            for o, w in (("QN", "IO"), ("XQ", "X")):
                act(A(o), IND(A(w, 0, W), A("QO")), AF.Copy)

        def marks():
            ts(A("QR", 0, 8), A("Q2"), col(C_RM), OP.add)
            ts(A("QR", 8, 16), A("Q2"), col(C_RM2), OP.add)

        def newz():
            mm(A("EX", 0, 128), A("nIb"), Z, True)
            mm(A("EX", 0, 128), A("Ib"), A("XQ"), False, True)
            search("s", 4, 3, 1, 0)
            act(A(O, 96, 224), A("EX", 0, 128), AF.Abs)
            for h in range(1 if last else 2):
                act(A("T1", 128 * h, 128 * h + 128), A("EX", 0, 128), bias=191.75, scale=0.5)

        def search(q, *which):
            for s in which:
                o, i = A("E", TRI[s], TRI[s + 1]), A("QN", 0, 16 * s + 16)
                if q == "s":
                    act(o, i, AF.Abs, bias=A("NB", s, s + 1), scale=FAR)
                else:
                    ts(o, i, A("QF", s, s + 1), OP.not_equal, FAR, OP.mult)

        def update(between):
            scan(A("ES"), A("DD"), A("E"), OP.add, OP.min)
            between[0]()
            tt(A("LO"), IND(A("ES"), L(L_END, 1)), A("QR"), OP.subtract)
            between[1]()
            tt(A("LO2"), A("LO"), A("DUM"), OP.max)
            between[2]()
            ts(A("SO"), A("LO2"), -1.0, OP.mult)
            between[3]()
            n = 8 if last else 16
            tt(IND(XW, A("SO", 0, n)), A("T1", 0, 16 * n), A("ZM", 0, 16 * n), OP.add)

        if not last:
            walk()
            tt(A("G2"), IND(A("NX"), A("QO")), A("MK"), OP.mult)
            newz()
            cp(A("QF"), A("Q2"))
            scan(A("SS", 0, 128), A("KP"), A("G2"), OP.mult, OP.add)
            search("v", 7)
            cp(A(O, 0, 48), IND(A("SS"), L(L_MSG, 3)))
            search("v", 6)
            tt(A(O, 48, 96), IND(A("SS"), L(L_MSG, 3)), A(O, 0, 48), OP.subtract)
            send(rank + 1, A("M%d" % (t + 1), 0, 224), A(O), "am%d" % (t + 1))
            send((rank ^ PX) + 1, A("PZ%d" % (t + 1)), A(O, 96, 224), "az%d" % (t + 1))
            search("v", 5, 2)
            marks()
            if t == 0:
                next_constants()
                reversals()
                lower()
                act(A("If"), A("Ib"))
                act(A("nIf"), A("Ib"), scale=-1.0)
            update([both_steps,
                    lambda: (prepare(t + 1), ts(A("PI", 0, 1), A("WL", 8, 9), 16.0 / 31.0, OP.mult, 16384.25, OP.add)),
                    lambda: ts(A("PI", 4, 5), A("PI", 0, 1), 1023, OP.bitwise_and),
                    lambda: ts(A("PN", 0, 1), A("PI", 4, 5), -1.0, OP.mult, 1919.0, OP.add)])
            act(A("D0", 16, 256, 32), A("QF"), bias=A("PN", 0, 1), scale=0.0)
        else:
            WF = "W%d" % RO
            walk()
            cp(A("QF"), A("Q2"))
            marks()
            ts(A("ta", 0, 192), A(WF, 8, 200), 0.25, OP.add)
            newz()
            send(rank ^ PX, A("PZ%d" % RO), A(O, 96, 224), "az%d" % RO)
            search("v", 7, 6, 5, 2)
            update([lambda: tt(A("fa", 0, 128), A(WF, 8, 136), A("ta", 0, 128), OP.is_lt),
                    lambda: (tt(A("fa", 128, 192), A(WF, 136, 200), A("ta", 128, 192), OP.is_lt),
                             ts(A("fb", 0, 128), A("fa", 0, 128), -4096.25, OP.mult)),
                    lambda: tt(A("U", 0, 128), A("fb", 0, 128), A(WF, 8, 136), OP.add),
                    lambda: ts(A("fb", 128, 192), A("fa", 128, 192), -4096.25, OP.mult)])
            dma("y", "dyx", H(T.yx[:]), A("X", 0, W))
            act(A("YC"), IND(A("NX"), A("QO")), bias=-0.25)
            dma("y", "dyz", H(T.yz[:]), A(O, 96, 224))
            dma("y", "dyc", H(T.yc[:]), A("YC", rows=slice(0, 128, 16)))
            tt(A("U", 128, 192), A("fb", 128, 192), A(WF, 136, 200), OP.add)
            cp(A("fc"), IND(A("U", 0, 128), L(L_I1, 16)))
            act(A("PL"), IND(A("U"), L(L_I3, 16)), AF.Copy)
            turn(A("fa"), A("fc"))
            turn(A("fb"), A("PL"))
            ex_diff(A(O, 96, 224), RO)
            act(A("G1"), IND(A("fa"), L(L_I2, 8)), AF.Abs, bias=-0.25, scale=2.0)
            ex_signs(lambda: act(A("G2"), IND(A("fb"), L(L_I2, 8)), AF.Abs, bias=-0.25, scale=2.0))
            mm(A("EX", 128, 256), A("BO"), A("S1"), True, True)
            tt(A("SS", 0, 128), A("G2"), A("G1"), OP.subtract)
            ts(A("F1a", 0, 128), A("EX", 128, 256), 1.0, OP.is_ge)
            tt(A("F1b", 0, 128), A("SS", 0, 128), A("F1a", 0, 128), OP.mult)
            tt(A("YH"), A("G1"), A("F1b", 0, 128), OP.add)
            dma("y", "dyh", H(T.yh[:]), A("YH"))

    for sem, n in cnt.items():
        g.wait_ge(T.sem[sem], n)
